import numpy as np
import ml_dtypes


def mxq(x, axis, fmt="e4m3"):
    dtype, down = {"e4m3": (ml_dtypes.float8_e4m3fn, 7), "e5m2": (ml_dtypes.float8_e5m2, 14)}[fmt]
    v = np.moveaxis(np.asarray(x, np.float32).astype(ml_dtypes.bfloat16).astype(np.float64), axis, -1)
    blocks = v.reshape(v.shape[:-1] + (-1, 32))
    amax = np.abs(blocks).max(-1, keepdims=True)
    byte = np.maximum(np.where(amax > 0, np.frexp(amax)[1] - 1 + 127, 0) - down, 1)
    scale = np.exp2(byte - 127.0)
    codes = (blocks / scale).astype(np.float32).astype(dtype).astype(np.float64)
    return np.moveaxis((codes * scale).reshape(v.shape), -1, axis)


WIDE = False


def mx_kscale(k):
    if not WIDE:
        return np.ones(k)
    levels = np.array([10, -10, 5, -5, 0])
    if k % 512:
        return np.exp2(np.random.permutation(np.resize(levels, k // 32))).repeat(32)
    a = np.empty((k // 512, 16))
    for p in range(k // 512):
        a[p, :8] = np.random.permutation(np.resize(levels, 8))
        for g in range(8):
            far = levels[np.abs(levels - a[p, g]) >= 10]
            a[p, g + 8] = far[np.random.randint(len(far))]
    return np.exp2(a.ravel()).repeat(32)


def f64(x):
    return np.asarray(x).astype(np.float64)


def striped(idx):
    return np.tile(idx.reshape(-1, 16).T, (8, 1)).astype(np.uint16)


def unstriped(offs):
    return offs[:16].T.reshape(-1).astype(np.int64)


def pack_weight(w):
    k, n = w.shape
    w = f64(np.asarray(w, np.float32).astype(ml_dtypes.bfloat16)).reshape(k // 32, 32, n)
    amax = np.abs(w).max(1)
    byte = np.clip(np.where(amax > 0, np.frexp(amax)[1] - 1 + 127 - 7, 1), 1, 254)
    scaled = (w * np.exp2(127.0 - byte)[:, None, :]).reshape(k, n).astype(np.float32)
    words = np.ascontiguousarray(scaled.reshape(k // 512, 128, 4, n).transpose(0, 1, 3, 2)).astype(ml_dtypes.float8_e4m3fn).view(np.uint8)
    return words, np.ascontiguousarray(byte.astype(np.uint8).reshape(k // 512, 16, n))


def unpack_weight(words, scales):
    g, p, n, _ = words.shape
    vals = np.ascontiguousarray(words).view(ml_dtypes.float8_e4m3fn).astype(np.float64) * np.repeat(np.exp2(scales.astype(np.float64) - 127.0), 8, axis=1)[..., None]
    return vals.transpose(0, 1, 3, 2).reshape(g * 512, n)


def relu(v):
    return np.maximum(v, 0.0)


def sigmoid(v):
    return 1.0 / (1.0 + np.exp(-np.maximum(v, -700.0)))


K, T, S, V, H, N = 512, 2048, 512, 256, 512, 512


def setup_inputs():
    n = np.random.standard_normal
    s = mx_kscale(K)[:, None]
    u = mx_kscale(H)
    near = np.random.permutation(S)
    packed_xT = pack_weight(n((K, T)) * s)
    return {
        "x_words": packed_xT[0],
        "x_scales": packed_xT[1],
        "w1": (n((K, N)) / np.sqrt(K) / s).astype(np.float32),
        "w2": (n((K, N)) / np.sqrt(K) / s).astype(np.float32),
        "w3": (n((K, N)) / np.sqrt(K) / s).astype(np.float32),
        "gain": (np.random.uniform(0.5, 1.5, (H, 1)) * u[:, None]).astype(np.float32),
        "m1": (n((H, N)) / np.sqrt(H) / u[:, None]).astype(np.float32),
        "m2": (n((H, N)) / np.sqrt(H) / u[:, None]).astype(np.float32),
        "m3": (n((H, N)) / np.sqrt(H) / u[:, None]).astype(np.float32),
        "offs": striped(np.random.permutation(T)[:S]),
        "pos1": striped(near[:V]),
        "pos2": striped(near[V:]),
        "own": striped(np.random.permutation(S)[:V]),
    }


def reference(x_words, x_scales, w1, w2, w3, gain, m1, m2, m3, offs, pos1, pos2, own):
    xq = unpack_weight(x_words, x_scales)[:, unstriped(offs)]
    y0 = mxq(f64(w1), 0, "e4m3").T @ xq
    lo = relu((y0[:, unstriped(pos1)] + y0[:, unstriped(pos2)]) / 2)
    z0 = f64(gain) * lo
    e0 = np.exp(sigmoid(mxq(f64(m1), 0, "e4m3").T @ mxq(z0, 0, "e4m3")))
    y1 = mxq(f64(w2), 0, "e4m3").T @ xq
    hi = relu(y1[:, unstriped(own)] - ((y1[:, unstriped(pos1)] + y1[:, unstriped(pos2)]) / 2))
    z1 = f64(gain) * hi
    e1 = np.exp(sigmoid(mxq(f64(m2), 0, "e4m3").T @ mxq(z1, 0, "e4m3")))
    y2 = mxq(f64(w3), 0, "e4m3").T @ xq
    se = relu(y2[:, unstriped(own)])
    z2 = f64(gain) * se
    e2 = np.exp(sigmoid(mxq(f64(m3), 0, "e4m3").T @ mxq(z2, 0, "e4m3")))
    num = lo * e0 + hi * e1 + se * e2
    den = e0 + e1 + e2
    return num / den

@@ -1,0 +1,268 @@
+from contextlib import ExitStack
+
+import concourse.mybir as mybir
+from concourse.masks import make_identity
+
+K, T, S, V, H, N = 512, 2048, 512, 256, 512, 512
+FLOPS = 2 * 3 * K * N * S + 2 * 3 * H * N * V
+
+F32 = mybir.dt.float32
+BF16 = mybir.dt.bfloat16
+I32 = mybir.dt.int32
+U32 = mybir.dt.uint32
+U16 = mybir.dt.uint16
+U8 = mybir.dt.uint8
+FP8X4 = mybir.dt.float8_e4m3fn_x4
+ALU = mybir.AluOpType
+ACT = mybir.ActivationFunctionType
+
+P = 128
+PACK = 4
+HALVES = V // P
+
+
+def tile_picked_yacm_mix_p_kernel(
+    tc, x_words, x_scales, w1, w2, w3, gain, m1, m2, m3, offs, pos1, pos2, own, out
+):
+    nc = tc.nc
+    with ExitStack() as ctx:
+        lists = ctx.enter_context(tc.tile_pool(name="lists", bufs=1))
+        keep = ctx.enter_context(tc.tile_pool(name="keep", bufs=1))
+        mm_banks = ctx.enter_context(tc.psum_pool(name="mm_banks", bufs=2))
+        turn_banks = ctx.enter_context(tc.psum_pool(name="turn_banks", bufs=2))
+        sum_banks = ctx.enter_context(tc.psum_pool(name="sum_banks", bufs=1))
+
+        def sb(name, shape, dtype, tag=None):
+            return keep.tile(shape, dtype, name=name, tag=tag or name, align_bytes=64)
+
+        def load_list(name, src):
+            tile = lists.tile([P, src.shape[1]], U16, name=name)
+            nc.sync.dma_start(out=tile[:], in_=src)
+            return tile
+
+        def load_rows(name, src, c0, c1):
+            raw = sb(name, [P, PACK, c1 - c0], F32)
+            nc.sync.dma_start(out=raw[:], in_=src.rearrange("(p j) c -> p j c", j=PACK)[:, :, c0:c1])
+            return raw
+
+        warm_in = sb("warm_in", [P, 1], F32)
+        warm_out = sb("warm_out", [P, 1], F32)
+        nc.vector.memset(warm_in[:], 0.0)
+        nc.scalar.activation(out=warm_out[:], in_=warm_in[:], func=ACT.Tanh)
+
+        scale_table = sb("scale_table", [P, T], U8)
+        nc.vector.memset(scale_table[:].bitcast(I32), 0)
+
+        scale_rows = sb("scale_rows", [P, T // 4], I32)
+        for q in range(4):
+            nc.sync.dma_start(out=scale_rows[32 * q : 32 * q + 4, :], in_=x_scales[0, 4 * q : 4 * q + 4, :].bitcast(I32))
+        offs_t = load_list("offs_t", offs)
+        word_table = sb("word_table", [P, T], U32)
+        nc.sync.dma_start(out=word_table[:].bitcast(I32), in_=x_words[0].rearrange("p n t -> p (n t)").bitcast(I32))
+        w_hi_raw = [load_rows("w_hi_raw%d" % i, w2, i * N // 2, (i + 1) * N // 2) for i in range(2)]
+        own_t = load_list("own_t", own)
+        pos1_t = load_list("pos1_t", pos1)
+        pos2_t = load_list("pos2_t", pos2)
+        w_lo_raw = load_rows("w_lo_raw", w1, 0, N)
+        w_se_raw = load_rows("w_se_raw", w3, 0, N)
+        gain_t = sb("gain_t", [P, PACK], F32)
+        nc.sync.dma_start(out=gain_t[:], in_=gain.rearrange("(p t) o -> p (t o)", t=PACK))
+        m_hi_raw = load_rows("m_hi_raw", m2, 0, N)
+        m_lo_raw = load_rows("m_lo_raw", m1, 0, N)
+        m_se_raw = load_rows("m_se_raw", m3, 0, N)
+
+        ident = sb("ident", [P, P], F32)
+        make_identity(nc, ident[:])
+
+        for q in range(4):
+            nc.vector.tensor_copy(out=scale_table[32 * q : 32 * q + 4, :].bitcast(I32), in_=scale_rows[32 * q : 32 * q + 4, :])
+        x_codes = sb("x_codes", [P, S], U32)
+        x_exps = sb("x_exps", [P, S], U8)
+        nc.vector.tensor_copy(out=x_exps[:], in_=scale_table[:].indirect(offs_t[:]))
+        nc.vector.tensor_copy(out=x_codes[:], in_=word_table[:].indirect(offs_t[:]))
+
+        def cast_w(copy, grouped, raw, m0):
+            cols = raw.shape[2] // PACK
+            copy(
+                out=grouped[:].rearrange("p (t m j) -> p m t j", t=PACK, j=PACK)[:, m0 : m0 + cols],
+                in_=raw[:].rearrange("p j (m t) -> p m t j", t=PACK),
+            )
+
+        def cast_m(copy, name, raw):
+            grouped = sb(name, [P, N * PACK], BF16)
+            copy(
+                out=grouped[:].rearrange("p (c i j) -> p c j i", i=4, j=PACK),
+                in_=raw[:].rearrange("p j (c i) -> p c j i", i=4),
+            )
+            return grouped
+
+        def mx_tiles(name, width):
+            return sb(name + "_codes", [P, width], U32), sb(name + "_exps", [P, width], U8)
+
+        def quantize(mx, grouped, c0, c1):
+            nc.vector.quantize_mx(
+                out=mx[0][:, c0:c1].bitcast(FP8X4), scales=mx[1][:, c0:c1], in_=grouped[:, PACK * c0 : PACK * c1]
+            )
+
+        def project(name, mx, t, func, scale):
+            bank = sum_banks.tile([P, S], F32, name="y_bank", tag="sum%d" % t)
+            cols = slice(t * P, (t + 1) * P)
+            nc.tensor.matmul_mx(
+                out=bank[:], lhsT=mx[0][:, cols].bitcast(FP8X4), lhsT_scale=mx[1][:, cols],
+                rhs=x_codes[:].bitcast(FP8X4), rhs_scale=x_exps[:], start=True, stop=True,
+            )
+            window = sb("%s_y%d" % (name, t), [P, S], F32)
+            nc.scalar.activation(out=window[:], in_=bank[:], func=func, scale=scale)
+            return window
+
+        def piece(tile, t):
+            return tile[:, t * V : (t + 1) * V]
+
+        def make_z(name, pre, h, tag=None):
+            z = sb("%s_z%d" % (name, h), [P, P * PACK], BF16, tag=tag)
+            nc.vector.scalar_tensor_tensor(
+                out=z[:].rearrange("p (v t) -> p v t", t=PACK),
+                in0=pre[:].rearrange("p (t v) -> p v t", t=PACK)[:, h * P : (h + 1) * P, :],
+                scalar=0.0,
+                in1=gain_t[:].rearrange("p (o t) -> p o t", o=1).to_broadcast([P, P, PACK]),
+                op0=ALU.max, op1=ALU.mult,
+            )
+            return z
+
+        def quantize_z(z, h, z_mx):
+            nc.vector.quantize_mx(
+                out=z_mx[0][:, h * P : (h + 1) * P].bitcast(FP8X4), scales=z_mx[1][:, h * P : (h + 1) * P], in_=z[:]
+            )
+
+        def weight(name, z_mx, m_mx, h):
+            bank = mm_banks.tile([P, N], F32, name="mm")
+            cols = slice(h * P, (h + 1) * P)
+            nc.tensor.matmul_mx(
+                out=bank[:], lhsT=z_mx[0][:, cols].bitcast(FP8X4), lhsT_scale=z_mx[1][:, cols],
+                rhs=m_mx[0][:].bitcast(FP8X4), rhs_scale=m_mx[1][:], start=True, stop=True,
+            )
+            th = sb("%s_th%d" % (name, h), [P, N], F32)
+            nc.scalar.activation(
+                out=th[:].rearrange("p (t m) -> p t m", t=PACK), in_=bank[:].rearrange("p (m t) -> p t m", t=PACK),
+                func=ACT.Tanh, scale=0.5,
+            )
+            e = sb("%s_e%d" % (name, h), [P, N], F32)
+            nc.scalar.activation(out=e[:], in_=th[:], func=ACT.Exp, scale=0.5)
+            return e
+
+
+        def turn_add(bank, src, first, last):
+            for t in range(PACK):
+                nc.tensor.matmul(
+                    out=bank[:, t * P : (t + 1) * P], lhsT=src[:, t * P : (t + 1) * P], rhs=ident[:],
+                    is_transpose=True, start=(first and t == 0), stop=(last and t == PACK - 1),
+                )
+
+        def mix(name, pre, e, h, first, last, tag=None):
+            turned = turn_banks.tile([P, N], F32, name="turned")
+            for t in range(PACK):
+                nc.tensor.transpose(turned[:, t * P : (t + 1) * P], pre[:, t * V + h * P : t * V + (h + 1) * P], ident[:])
+            turn_add(den[h], e, first, last)
+            prod = sb("%s_p%d" % (name, h), [P, N], F32, tag=tag)
+            nc.vector.scalar_tensor_tensor(
+                out=prod[:], in0=turned[:], scalar=0.0, in1=e[:], op0=ALU.max, op1=ALU.mult
+            )
+            turn_add(num[h], prod, first, last)
+
+        w_hi_bf = sb("w_hi_bf", [P, N * PACK], BF16)
+        cast_w(nc.scalar.copy, w_hi_bf, w_hi_raw[0], 0)
+        cast_w(nc.vector.tensor_copy, w_hi_bf, w_hi_raw[1], P // 2)
+        w_hi = mx_tiles("w_hi", N)
+        y_hi = []
+        for t in range(PACK):
+            quantize(w_hi, w_hi_bf, t * P, (t + 1) * P)
+            y_hi.append(project("hi", w_hi, t, ACT.Copy, -0.5))
+
+        hi_own = sb("hi_own", [P, PACK * V], F32)
+        hi_own2 = sb("hi_own2", [P, PACK * V], F32)
+        hi_part = sb("hi_part", [P, PACK * V], F32)
+        for t in range(PACK):
+            nc.vector.tensor_copy(out=piece(hi_own, t), in_=y_hi[t][:].indirect(own_t[:]))
+            if t % 2 == 1:
+                cols = slice((t - 1) * V, (t + 1) * V)
+                nc.scalar.activation(out=hi_own2[:, cols], in_=hi_own[:, cols], func=ACT.Copy, scale=2.0)
+        w_lo_bf = sb("w_lo_bf", [P, N * PACK], BF16)
+        cast_w(nc.scalar.copy, w_lo_bf, w_lo_raw, 0)
+        for t in range(PACK):
+            nc.vector.tensor_tensor(
+                out=piece(hi_part, t), in0=y_hi[t][:].indirect(pos1_t[:]), in1=piece(hi_own2, t), op=ALU.subtract
+            )
+        w_lo = mx_tiles("w_lo", N)
+        quantize(w_lo, w_lo_bf, 0, N)
+        w_se_bf = sb("w_se_bf", [P, N * PACK], BF16)
+        cast_w(nc.scalar.copy, w_se_bf, w_se_raw, 0)
+        y_lo = [project("lo", w_lo, t, ACT.Copy, 0.5) for t in range(PACK)]
+        hi_pre = sb("hi_pre", [P, PACK * V], F32, tag="w_lo_bf")
+        for t in range(PACK):
+            nc.vector.tensor_tensor(
+                out=piece(hi_pre, t), in0=y_hi[t][:].indirect(pos2_t[:]), in1=piece(hi_part, t), op=ALU.add
+            )
+        w_se = mx_tiles("w_se", N)
+        quantize(w_se, w_se_bf, 0, N)
+        m_hi_bf = cast_m(nc.scalar.copy, "m_hi_bf", m_hi_raw)
+        y_se = [project("se", w_se, t, ACT.Relu, 1.0) for t in range(PACK)]
+        num = [sum_banks.tile([P, PACK * P], F32, name="num%d" % h, tag="sum%d" % h) for h in range(HALVES)]
+        den = [sum_banks.tile([P, PACK * P], F32, name="den%d" % h, tag="sum%d" % (2 + h)) for h in range(HALVES)]
+        z_hi_mx = mx_tiles("z_hi", V)
+        z_hi = [make_z("hi", hi_pre, 0, "w_se_bf"), make_z("hi", hi_pre, 1)]
+        m_hi = mx_tiles("m_hi", N)
+        quantize(m_hi, m_hi_bf, 0, N)
+        for h in range(HALVES):
+            quantize_z(z_hi[h], h, z_hi_mx)
+        e_hi = [weight("hi", z_hi_mx, m_hi, h) for h in range(HALVES)]
+        m_lo_bf = cast_m(nc.scalar.copy, "m_lo_bf", m_lo_raw)
+        lo_part = sb("lo_part", [P, PACK * V], F32, tag="m_hi_bf")
+        for t in range(PACK):
+            nc.vector.tensor_copy(out=piece(lo_part, t), in_=y_lo[t][:].indirect(pos1_t[:]))
+        lo_pre = sb("lo_pre", [P, PACK * V], F32)
+        for t in range(PACK):
+            nc.vector.tensor_tensor(
+                out=piece(lo_pre, t), in0=y_lo[t][:].indirect(pos2_t[:]), in1=piece(lo_part, t), op=ALU.add
+            )
+        m_se_bf = cast_m(nc.scalar.copy, "m_se_bf", m_se_raw)
+        z_lo_mx = mx_tiles("z_lo", V)
+        m_lo = mx_tiles("m_lo", N)
+        quantize(m_lo, m_lo_bf, 0, N)
+        z_lo = [make_z("lo", lo_pre, 0, "m_lo_bf"), make_z("lo", lo_pre, 1)]
+        for h in range(HALVES):
+            quantize_z(z_lo[h], h, z_lo_mx)
+        e_lo = [weight("lo", z_lo_mx, m_lo, h) for h in range(HALVES)]
+        for h in range(HALVES):
+            mix("hi", hi_pre, e_hi[h], h, True, False)
+
+        m_se = mx_tiles("m_se", N)
+        quantize(m_se, m_se_bf, 0, N)
+        se_pre = sb("se_pre", [P, PACK * V], F32, tag="m_se_bf")
+        z_se_mx = mx_tiles("z_se", V)
+        e_se = []
+        for h in range(HALVES):
+            for t in range(PACK):
+                nc.vector.tensor_copy(
+                    out=se_pre[:, t * V + h * P : t * V + (h + 1) * P],
+                    in_=y_se[t][:].indirect(own_t[:, h * P // 16 : (h + 1) * P // 16]),
+                )
+            quantize_z(make_z("se", se_pre, h), h, z_se_mx)
+            e_se.append(weight("se", z_se_mx, m_se, h))
+        for h in range(HALVES):
+            mix("lo", lo_pre, e_lo[h], h, False, False, "se_z%d" % (1 - h))
+        for h in range(HALVES):
+            mix("se", se_pre, e_se[h], h, False, True)
+
+        out_rows = out.rearrange("(p t) v -> p t v", t=PACK)
+        for h in range(HALVES):
+            root = sb("root%d" % h, [P, PACK * P], F32, tag="se_th%d" % (1 - h))
+            nc.scalar.activation(out=root[:], in_=den[h][:], func=ACT.Abs_reciprocal_sqrt)
+            once = sb("once%d" % h, [P, PACK * P], F32)
+            res = sb("res%d" % h, [P, PACK * P], F32)
+            if h == 0:
+                nc.vector.tensor_tensor(out=once[:], in0=num[h][:], in1=root[:], op=ALU.mult)
+                nc.vector.tensor_tensor(out=res[:], in0=once[:], in1=root[:], op=ALU.mult)
+            else:
+                nc.scalar.activation(out=once[:], in_=root[:], func=ACT.Square)
+                nc.vector.tensor_tensor(out=res[:], in0=num[h][:], in1=once[:], op=ALU.mult)
+            nc.sync.dma_start(out=out_rows[:, :, h * P : (h + 1) * P], in_=res[:].rearrange("p (t v) -> p t v", t=PACK))

@@ -57,19 +57,21 @@ def tile_picked_yacm_mix_p_kernel(
         for q in range(4):
             nc.sync.dma_start(out=scale_rows[32 * q : 32 * q + 4, :], in_=x_scales[0, 4 * q : 4 * q + 4, :].bitcast(I32))
         offs_t = load_list("offs_t", offs)
+        gain_t = sb("gain_t", [P, PACK], F32)
+        nc.sync.dma_start(out=gain_t[:], in_=gain.rearrange("(p t) o -> p (t o)", t=PACK))
+        w_hi_cuts = [0, P, 2 * P, N]
+        w_hi_raw = [load_rows("w_hi_raw0", w2, 0, w_hi_cuts[1])] if False else []
         word_table = sb("word_table", [P, T], U32)
         nc.sync.dma_start(out=word_table[:].bitcast(I32), in_=x_words[0].rearrange("p n t -> p (n t)").bitcast(I32))
-        w_hi_raw = [load_rows("w_hi_raw%d" % i, w2, i * N // 2, (i + 1) * N // 2) for i in range(2)]
+        w_hi_raw += [load_rows("w_hi_raw%d" % c0, w2, c0, c1) for c0, c1 in list(zip(w_hi_cuts, w_hi_cuts[1:]))[len(w_hi_raw):]]
         own_t = load_list("own_t", own)
         pos1_t = load_list("pos1_t", pos1)
         pos2_t = load_list("pos2_t", pos2)
-        w_lo_raw = load_rows("w_lo_raw", w1, 0, N)
         w_se_raw = load_rows("w_se_raw", w3, 0, N)
-        gain_t = sb("gain_t", [P, PACK], F32)
-        nc.sync.dma_start(out=gain_t[:], in_=gain.rearrange("(p t) o -> p (t o)", t=PACK))
+        w_lo_raw = load_rows("w_lo_raw", w1, 0, N)
         m_hi_raw = load_rows("m_hi_raw", m2, 0, N)
-        m_lo_raw = load_rows("m_lo_raw", m1, 0, N)
         m_se_raw = load_rows("m_se_raw", m3, 0, N)
+        m_lo_raw = load_rows("m_lo_raw", m1, 0, N)
 
         ident = sb("ident", [P, P], F32)
         make_identity(nc, ident[:])
@@ -81,61 +83,94 @@ def tile_picked_yacm_mix_p_kernel(
         nc.vector.tensor_copy(out=x_exps[:], in_=scale_table[:].indirect(offs_t[:]))
         nc.vector.tensor_copy(out=x_codes[:], in_=word_table[:].indirect(offs_t[:]))
 
-        def cast_w(copy, grouped, raw, m0):
-            cols = raw.shape[2] // PACK
+        def gpsimd_cast(out, in_):
+            for j in range(1):
+                nc.gpsimd.tensor_scalar(out=out, in0=in_, scalar1=1.0, scalar2=0.0, op0=ALU.mult, op1=ALU.add)
+
+        def cast_dealt(copy, name, raw, tag=None):
+            grouped = sb(name, [P, N * PACK], BF16, tag=tag)
             copy(
-                out=grouped[:].rearrange("p (t m j) -> p m t j", t=PACK, j=PACK)[:, m0 : m0 + cols],
+                out=grouped[:].rearrange("p (t m j) -> p m t j", t=PACK, j=PACK),
                 in_=raw[:].rearrange("p j (m t) -> p m t j", t=PACK),
             )
+            return grouped
 
-        def cast_m(copy, name, raw):
-            grouped = sb(name, [P, N * PACK], BF16)
+        def cast(copy, name, raw, c0=0, c1=None, tag=None):
+            c1 = c1 or raw.shape[2]
+            grouped = sb(name, [P, (c1 - c0) * PACK], BF16, tag=tag)
             copy(
                 out=grouped[:].rearrange("p (c i j) -> p c j i", i=4, j=PACK),
-                in_=raw[:].rearrange("p j (c i) -> p c j i", i=4),
+                in_=raw[:, :, c0:c1].rearrange("p j (c i) -> p c j i", i=4),
             )
             return grouped
 
         def mx_tiles(name, width):
             return sb(name + "_codes", [P, width], U32), sb(name + "_exps", [P, width], U8)
 
-        def quantize(mx, grouped, c0, c1):
-            nc.vector.quantize_mx(
-                out=mx[0][:, c0:c1].bitcast(FP8X4), scales=mx[1][:, c0:c1], in_=grouped[:, PACK * c0 : PACK * c1]
-            )
+        def quantize(mx, c0, grouped):
+            c1 = c0 + grouped.shape[1] // PACK
+            nc.vector.quantize_mx(out=mx[0][:, c0:c1].bitcast(FP8X4), scales=mx[1][:, c0:c1], in_=grouped[:])
 
-        def project(name, mx, t, func, scale):
+        def project(name, mx, t, func, scale, tag=None):
             bank = sum_banks.tile([P, S], F32, name="y_bank", tag="sum%d" % t)
             cols = slice(t * P, (t + 1) * P)
             nc.tensor.matmul_mx(
                 out=bank[:], lhsT=mx[0][:, cols].bitcast(FP8X4), lhsT_scale=mx[1][:, cols],
                 rhs=x_codes[:].bitcast(FP8X4), rhs_scale=x_exps[:], start=True, stop=True,
             )
-            window = sb("%s_y%d" % (name, t), [P, S], F32)
+            window = sb("%s_y%d" % (name, t), [P, S], F32, tag=tag)
             nc.scalar.activation(out=window[:], in_=bank[:], func=func, scale=scale)
             return window
 
-        def piece(tile, t):
-            return tile[:, t * V : (t + 1) * V]
+        def gather(dst, windows, t, offsets, h=None):
+            if h is None:
+                nc.vector.tensor_copy(out=dst[:, t * V : (t + 1) * V], in_=windows[t][:].indirect(offsets[:]))
+            else:
+                nc.vector.tensor_copy(
+                    out=dst[:, t * V + h * P : t * V + (h + 1) * P],
+                    in_=windows[t][:].indirect(offsets[:, h * P // 16 : (h + 1) * P // 16]),
+                )
 
-        def make_z(name, pre, h, tag=None):
+        def direct_z(name, pre, h, tag=None):
             z = sb("%s_z%d" % (name, h), [P, P * PACK], BF16, tag=tag)
             nc.vector.scalar_tensor_tensor(
                 out=z[:].rearrange("p (v t) -> p v t", t=PACK),
-                in0=pre[:].rearrange("p (t v) -> p v t", t=PACK)[:, h * P : (h + 1) * P, :],
+                in0=pre[:].rearrange("p (t v) -> p v t", t=PACK),
                 scalar=0.0,
                 in1=gain_t[:].rearrange("p (o t) -> p o t", o=1).to_broadcast([P, P, PACK]),
                 op0=ALU.max, op1=ALU.mult,
             )
             return z
 
-        def quantize_z(z, h, z_mx):
-            nc.vector.quantize_mx(
-                out=z_mx[0][:, h * P : (h + 1) * P].bitcast(FP8X4), scales=z_mx[1][:, h * P : (h + 1) * P], in_=z[:]
+        def plain(bank):
+            return bank[:].rearrange("p (t m) -> p t m", t=PACK)
+
+        def turn_sum(terms, h, pool=turn_banks, tag="turn"):
+            bank = pool.tile([P, N], F32, name="turned", tag="%s%d" % (tag, h), bufs=1)
+            for i, term in enumerate(terms):
+                for t in range(PACK):
+                    nc.tensor.matmul(
+                        out=bank[:, t * P : (t + 1) * P], lhsT=term.rearrange("p (t v) -> p t v", t=PACK)[:, t, h * P % (term.shape[1] // PACK) :][:, :P], rhs=ident[:],
+                        is_transpose=True, start=(i == 0 and t == 0), stop=(i == len(terms) - 1 and t == PACK - 1),
+                    )
+            return bank
+
+        def turned_z(name, turned, h, tag=None):
+            zt = sb("%s_zt%d" % (name, h), [P, N], BF16, tag=tag)
+            nc.vector.scalar_tensor_tensor(
+                out=zt[:], in0=turned[:], scalar=0.0, in1=gain_row[:], op0=ALU.max, op1=ALU.mult
             )
+            bank = mm_banks.tile([P, 2 * P], F32, name="pairs", tag="mm%d" % h, bufs=1)
+            for u in range(2):
+                nc.tensor.transpose(bank[:, u * P : (u + 1) * P], zt[:].bitcast(F32)[:, u : N // 2 : 2], ident[:])
+            z = sb("%s_z%d" % (name, h), [P, P * PACK], BF16)
+            nc.scalar.copy(
+                out=z[:].bitcast(F32).rearrange("p (v u) -> p v u", u=2), in_=bank[:].rearrange("p (u v) -> p v u", u=2)
+            )
+            return z
 
         def weight(name, z_mx, m_mx, h):
-            bank = mm_banks.tile([P, N], F32, name="mm")
+            bank = mm_banks.tile([P, N], F32, name="mm", tag="mm%d" % h, bufs=1)
             cols = slice(h * P, (h + 1) * P)
             nc.tensor.matmul_mx(
                 out=bank[:], lhsT=z_mx[0][:, cols].bitcast(FP8X4), lhsT_scale=z_mx[1][:, cols],
@@ -150,7 +185,6 @@ def tile_picked_yacm_mix_p_kernel(
             nc.scalar.activation(out=e[:], in_=th[:], func=ACT.Exp, scale=0.5)
             return e
 
-
         def turn_add(bank, src, first, last):
             for t in range(PACK):
                 nc.tensor.matmul(
@@ -158,104 +192,121 @@ def tile_picked_yacm_mix_p_kernel(
                     is_transpose=True, start=(first and t == 0), stop=(last and t == PACK - 1),
                 )
 
-        def mix(name, pre, e, h, first, last, tag=None):
-            turned = turn_banks.tile([P, N], F32, name="turned")
-            for t in range(PACK):
-                nc.tensor.transpose(turned[:, t * P : (t + 1) * P], pre[:, t * V + h * P : t * V + (h + 1) * P], ident[:])
-            turn_add(den[h], e, first, last)
+        def mix(name, turned, e, h, tag=None):
             prod = sb("%s_p%d" % (name, h), [P, N], F32, tag=tag)
             nc.vector.scalar_tensor_tensor(
-                out=prod[:], in0=turned[:], scalar=0.0, in1=e[:], op0=ALU.max, op1=ALU.mult
+                out=prod[:].rearrange("p (t m) -> p t m", t=PACK), in0=turned, scalar=0.0,
+                in1=e[:].rearrange("p (t m) -> p t m", t=PACK), op0=ALU.max, op1=ALU.mult,
             )
-            turn_add(num[h], prod, first, last)
+            return prod
 
-        w_hi_bf = sb("w_hi_bf", [P, N * PACK], BF16)
-        cast_w(nc.scalar.copy, w_hi_bf, w_hi_raw[0], 0)
-        cast_w(nc.vector.tensor_copy, w_hi_bf, w_hi_raw[1], P // 2)
+        def dealt(bank):
+            return bank[:].rearrange("p (m t) -> p t m", t=PACK)
+
+        gain_bank = mm_banks.tile([P, N], F32, name="gain_bank", tag="mm0", bufs=1)
+        for t in range(PACK):
+            nc.tensor.transpose(gain_bank[:, t * P : (t + 1) * P], gain_t[:, t : t + 1].to_broadcast([P, P]), ident[:])
+
+        gain_row = sb("gain_row", [P, N], F32)
+        nc.scalar.copy(out=gain_row[:].rearrange("p (m t) -> p m t", t=PACK), in_=gain_bank[:].rearrange("p (t m) -> p m t", t=PACK))
+
         w_hi = mx_tiles("w_hi", N)
         y_hi = []
-        for t in range(PACK):
-            quantize(w_hi, w_hi_bf, t * P, (t + 1) * P)
-            y_hi.append(project("hi", w_hi, t, ACT.Copy, -0.5))
+        for c0, raw in zip(w_hi_cuts, w_hi_raw):
+            for c in range(0, raw.shape[2], P):
+                t = (c0 + c) // P
+                quantize(w_hi, c0 + c, cast(nc.scalar.copy if t < 2 else nc.vector.tensor_copy, "w_hi_bf%d" % t, raw, c, c + P))
+                y_hi.append(project("hi", w_hi, t, ACT.Copy, -0.5))
 
+        hi_a = sb("hi_a", [P, PACK * V], F32)
         hi_own = sb("hi_own", [P, PACK * V], F32)
         hi_own2 = sb("hi_own2", [P, PACK * V], F32)
-        hi_part = sb("hi_part", [P, PACK * V], F32)
         for t in range(PACK):
-            nc.vector.tensor_copy(out=piece(hi_own, t), in_=y_hi[t][:].indirect(own_t[:]))
-            if t % 2 == 1:
-                cols = slice((t - 1) * V, (t + 1) * V)
-                nc.scalar.activation(out=hi_own2[:, cols], in_=hi_own[:, cols], func=ACT.Copy, scale=2.0)
-        w_lo_bf = sb("w_lo_bf", [P, N * PACK], BF16)
-        cast_w(nc.scalar.copy, w_lo_bf, w_lo_raw, 0)
-        for t in range(PACK):
-            nc.vector.tensor_tensor(
-                out=piece(hi_part, t), in0=y_hi[t][:].indirect(pos1_t[:]), in1=piece(hi_own2, t), op=ALU.subtract
-            )
-        w_lo = mx_tiles("w_lo", N)
-        quantize(w_lo, w_lo_bf, 0, N)
-        w_se_bf = sb("w_se_bf", [P, N * PACK], BF16)
-        cast_w(nc.scalar.copy, w_se_bf, w_se_raw, 0)
-        y_lo = [project("lo", w_lo, t, ACT.Copy, 0.5) for t in range(PACK)]
-        hi_pre = sb("hi_pre", [P, PACK * V], F32, tag="w_lo_bf")
-        for t in range(PACK):
-            nc.vector.tensor_tensor(
-                out=piece(hi_pre, t), in0=y_hi[t][:].indirect(pos2_t[:]), in1=piece(hi_part, t), op=ALU.add
-            )
+            gather(hi_own, y_hi, t, own_t)
+            gather(hi_a, y_hi, t, pos1_t)
+        w_se_bf = cast_dealt(nc.scalar.copy, "w_se_bf", w_se_raw)
+        w_lo_bf = cast_dealt(nc.scalar.copy, "w_lo_bf", w_lo_raw)
+        nc.scalar.activation(out=hi_own2[:], in_=hi_own[:], func=ACT.Copy, scale=-2.0)
         w_se = mx_tiles("w_se", N)
-        quantize(w_se, w_se_bf, 0, N)
-        m_hi_bf = cast_m(nc.scalar.copy, "m_hi_bf", m_hi_raw)
+        quantize(w_se, 0, w_se_bf)
         y_se = [project("se", w_se, t, ACT.Relu, 1.0) for t in range(PACK)]
+        hi_b = sb("hi_b", [P, PACK * V], F32, tag="w_se_bf")
+        for t in range(PACK):
+            gather(hi_b, y_hi, t, pos2_t)
+        hi_turned = [turn_sum([hi_a[:], hi_own2[:], hi_b[:]], h) for h in range(HALVES)]
+        w_lo = mx_tiles("w_lo", N)
+        quantize(w_lo, 0, w_lo_bf)
+        se = sb("se", [P, PACK * V], F32, tag="w_lo_bf")
+        for t in range(PACK):
+            gather(se, y_se, t, own_t)
+        m_hi_bf = cast(nc.scalar.copy, "m_hi_bf", m_hi_raw, 0, N, None)
+        m_se_bf = cast(nc.vector.tensor_copy, "m_se_bf", m_se_raw, 0, N, "se_y3")
+        z_hi = [turned_z("hi", hi_turned[h], h, ["se_y1", "se_y2"][h]) for h in range(HALVES)]
+        y_lo = [project("lo", w_lo, t, ACT.Copy, 0.5, "m_hi_raw" if t == 0 else None) for t in range(PACK)]
+        z_se = sb("se_z", [P, V * PACK], BF16, tag="gain_row")
+        nc.vector.tensor_tensor(
+            out=z_se[:].rearrange("p (c i t) -> p c t i", i=4, t=PACK),
+            in0=se[:].rearrange("p (t c i) -> p c t i", t=PACK, i=4),
+            in1=gain_t[:].rearrange("p (c t i) -> p c t i", c=1, i=1).to_broadcast([P, V // 4, PACK, 4]),
+            op=ALU.mult,
+        )
+        m_hi = mx_tiles("m_hi", N)
+        quantize(m_hi, 0, m_hi_bf)
+        z_hi_mx = mx_tiles("z_hi", V)
+        for h in range(HALVES):
+            quantize(z_hi_mx, h * P, z_hi[h])
+        z_se_mx = mx_tiles("z_se", V)
+        quantize(z_se_mx, 0, z_se)
+        m_se = mx_tiles("m_se", N)
+        quantize(m_se, 0, m_se_bf)
         num = [sum_banks.tile([P, PACK * P], F32, name="num%d" % h, tag="sum%d" % h) for h in range(HALVES)]
         den = [sum_banks.tile([P, PACK * P], F32, name="den%d" % h, tag="sum%d" % (2 + h)) for h in range(HALVES)]
-        z_hi_mx = mx_tiles("z_hi", V)
-        z_hi = [make_z("hi", hi_pre, 0, "w_se_bf"), make_z("hi", hi_pre, 1)]
-        m_hi = mx_tiles("m_hi", N)
-        quantize(m_hi, m_hi_bf, 0, N)
-        for h in range(HALVES):
-            quantize_z(z_hi[h], h, z_hi_mx)
         e_hi = [weight("hi", z_hi_mx, m_hi, h) for h in range(HALVES)]
-        m_lo_bf = cast_m(nc.scalar.copy, "m_lo_bf", m_lo_raw)
-        lo_part = sb("lo_part", [P, PACK * V], F32, tag="m_hi_bf")
-        for t in range(PACK):
-            nc.vector.tensor_copy(out=piece(lo_part, t), in_=y_lo[t][:].indirect(pos1_t[:]))
-        lo_pre = sb("lo_pre", [P, PACK * V], F32)
-        for t in range(PACK):
-            nc.vector.tensor_tensor(
-                out=piece(lo_pre, t), in0=y_lo[t][:].indirect(pos2_t[:]), in1=piece(lo_part, t), op=ALU.add
-            )
-        m_se_bf = cast_m(nc.scalar.copy, "m_se_bf", m_se_raw)
-        z_lo_mx = mx_tiles("z_lo", V)
-        m_lo = mx_tiles("m_lo", N)
-        quantize(m_lo, m_lo_bf, 0, N)
-        z_lo = [make_z("lo", lo_pre, 0, "m_lo_bf"), make_z("lo", lo_pre, 1)]
-        for h in range(HALVES):
-            quantize_z(z_lo[h], h, z_lo_mx)
-        e_lo = [weight("lo", z_lo_mx, m_lo, h) for h in range(HALVES)]
-        for h in range(HALVES):
-            mix("hi", hi_pre, e_hi[h], h, True, False)
+        e_se = [weight("se", z_se_mx, m_se, h) for h in range(HALVES)]
+        m_lo_bf = cast(nc.scalar.copy, "m_lo_bf", m_lo_raw, 0, N, "se_th0")
 
-        m_se = mx_tiles("m_se", N)
-        quantize(m_se, m_se_bf, 0, N)
-        se_pre = sb("se_pre", [P, PACK * V], F32, tag="m_se_bf")
-        z_se_mx = mx_tiles("z_se", V)
-        e_se = []
-        for h in range(HALVES):
+        lo_a = sb("lo_a", [P, PACK * V], F32, tag="gain_row")
+        for t in range(PACK):
+            gather(lo_a, y_lo, t, pos1_t)
+
+        def lo_sum(h, tag):
+            pre = sb("lo_pre%d" % h, [P, PACK * P], F32, tag=tag)
             for t in range(PACK):
-                nc.vector.tensor_copy(
-                    out=se_pre[:, t * V + h * P : t * V + (h + 1) * P],
-                    in_=y_se[t][:].indirect(own_t[:, h * P // 16 : (h + 1) * P // 16]),
+                nc.vector.tensor_tensor(
+                    out=pre[:, t * P : (t + 1) * P], in0=y_lo[t][:].indirect(pos2_t[:, h * P // 16 : (h + 1) * P // 16]),
+                    in1=lo_a[:, t * V + h * P : t * V + (h + 1) * P], op=ALU.add,
                 )
-            quantize_z(make_z("se", se_pre, h), h, z_se_mx)
-            e_se.append(weight("se", z_se_mx, m_se, h))
+            return pre
+
+        lo_pre = [lo_sum(0, None)]
+        z_lo_mx = mx_tiles("z_lo", V)
+        z_lo = direct_z("lo", lo_pre[0], 0, None)
+        p_hi = [mix("hi", dealt(hi_turned[h]), e_hi[h], h) for h in range(HALVES)]
+        quantize(z_lo_mx, 0, z_lo)
+        se_turned = [turn_sum([se[:]], h) for h in range(HALVES)]
         for h in range(HALVES):
-            mix("lo", lo_pre, e_lo[h], h, False, False, "se_z%d" % (1 - h))
+            turn_add(den[h], e_hi[h], True, False)
+        lo_pre.append(lo_sum(1, None))
+        m_lo = mx_tiles("m_lo", N)
+        quantize(m_lo, 0, m_lo_bf)
+        e_lo = [weight("lo", z_lo_mx, m_lo, 0)]
+        quantize(z_lo_mx, P, direct_z("lo", lo_pre[1], 1, "se_th0"))
+        e_lo.append(weight("lo", z_lo_mx, m_lo, 1))
         for h in range(HALVES):
-            mix("se", se_pre, e_se[h], h, False, True)
+            turn_add(num[h], p_hi[h], True, False)
+            turn_add(den[h], e_se[h], False, False)
+        p_se = [mix("se", plain(se_turned[h]), e_se[h], h, ["se_th0", "lo_z0"][h]) for h in range(HALVES)]
+        lo_turned = [turn_sum([lo_pre[h][:]], h, mm_banks, "mm") for h in range(HALVES)]
+        for h in range(HALVES):
+            turn_add(den[h], e_lo[h], False, True)
+            turn_add(num[h], p_se[h], False, False)
+        for h in range(HALVES):
+            p_lo = mix("lo", plain(lo_turned[h]), e_lo[h], h)
+            turn_add(num[h], p_lo, False, True)
 
         out_rows = out.rearrange("(p t) v -> p t v", t=PACK)
         for h in range(HALVES):
-            root = sb("root%d" % h, [P, PACK * P], F32, tag="se_th%d" % (1 - h))
+            root = sb("root%d" % h, [P, PACK * P], F32, tag="lo_th%d" % (1 - h))
             nc.scalar.activation(out=root[:], in_=den[h][:], func=ACT.Abs_reciprocal_sqrt)
             once = sb("once%d" % h, [P, PACK * P], F32)
             res = sb("res%d" % h, [P, PACK * P], F32)

@@ -32,7 +32,11 @@ def tile_picked_yacm_mix_p_kernel(
         turn_banks = ctx.enter_context(tc.psum_pool(name="turn_banks", bufs=2))
         sum_banks = ctx.enter_context(tc.psum_pool(name="sum_banks", bufs=1))
 
+        overlaid = ctx.enter_context(tc.tile_pool(name="overlaid", bufs=1))
+
         def sb(name, shape, dtype, tag=None):
+            if isinstance(tag, int):
+                return overlaid.tile(shape, dtype, name=name, align_bytes=64, offset=tag)
             return keep.tile(shape, dtype, name=name, tag=tag or name, align_bytes=64)
 
         def load_list(name, src):
@@ -40,8 +44,8 @@ def tile_picked_yacm_mix_p_kernel(
             nc.sync.dma_start(out=tile[:], in_=src)
             return tile
 
-        def load_rows(name, src, c0, c1):
-            raw = sb(name, [P, PACK, c1 - c0], F32)
+        def load_rows(name, src, c0, c1, tag=None):
+            raw = sb(name, [P, PACK, c1 - c0], F32, tag=tag)
             nc.sync.dma_start(out=raw[:], in_=src.rearrange("(p j) c -> p j c", j=PACK)[:, :, c0:c1])
             return raw
 
@@ -68,10 +72,10 @@ def tile_picked_yacm_mix_p_kernel(
         pos1_t = load_list("pos1_t", pos1)
         pos2_t = load_list("pos2_t", pos2)
         w_se_raw = load_rows("w_se_raw", w3, 0, N)
-        w_lo_raw = load_rows("w_lo_raw", w1, 0, N)
+        w_lo_raw = load_rows("w_lo_raw", w1, 0, N, 0)
         m_hi_raw = load_rows("m_hi_raw", m2, 0, N)
-        m_se_raw = load_rows("m_se_raw", m3, 0, N)
-        m_lo_raw = load_rows("m_lo_raw", m1, 0, N)
+        m_se_raw = load_rows("m_se_raw", m3, 0, N, 12288)
+        m_lo_raw = load_rows("m_lo_raw", m1, 0, N, 20480)
 
         ident = sb("ident", [P, P], F32)
         make_identity(nc, ident[:])
@@ -84,8 +88,10 @@ def tile_picked_yacm_mix_p_kernel(
         nc.vector.tensor_copy(out=x_codes[:], in_=word_table[:].indirect(offs_t[:]))
 
         def gpsimd_cast(out, in_):
-            for j in range(1):
-                nc.gpsimd.tensor_scalar(out=out, in0=in_, scalar1=1.0, scalar2=0.0, op0=ALU.mult, op1=ALU.add)
+            half = out.shape[1] // 2
+            for i in range(2):
+                cols = slice(i * half, (i + 1) * half)
+                nc.gpsimd.tensor_scalar(out=out[:, cols], in0=in_[:, cols], scalar1=1.0, scalar2=0.0, op0=ALU.mult, op1=ALU.add)
 
         def cast_dealt(copy, name, raw, tag=None):
             grouped = sb(name, [P, N * PACK], BF16, tag=tag)
@@ -163,7 +169,7 @@ def tile_picked_yacm_mix_p_kernel(
             bank = mm_banks.tile([P, 2 * P], F32, name="pairs", tag="mm%d" % h, bufs=1)
             for u in range(2):
                 nc.tensor.transpose(bank[:, u * P : (u + 1) * P], zt[:].bitcast(F32)[:, u : N // 2 : 2], ident[:])
-            z = sb("%s_z%d" % (name, h), [P, P * PACK], BF16)
+            z = sb("%s_z%d" % (name, h), [P, P * PACK], BF16, tag=[None, 32256][h])
             nc.scalar.copy(
                 out=z[:].bitcast(F32).rearrange("p (v u) -> p v u", u=2), in_=bank[:].rearrange("p (u v) -> p v u", u=2)
             )
@@ -217,55 +223,55 @@ def tile_picked_yacm_mix_p_kernel(
                 t = (c0 + c) // P
                 quantize(w_hi, c0 + c, cast(nc.scalar.copy if t < 2 else nc.vector.tensor_copy, "w_hi_bf%d" % t, raw, c, c + P))
                 y_hi.append(project("hi", w_hi, t, ACT.Copy, -0.5))
-
         hi_a = sb("hi_a", [P, PACK * V], F32)
         hi_own = sb("hi_own", [P, PACK * V], F32)
-        hi_own2 = sb("hi_own2", [P, PACK * V], F32)
         for t in range(PACK):
             gather(hi_own, y_hi, t, own_t)
             gather(hi_a, y_hi, t, pos1_t)
-        w_se_bf = cast_dealt(nc.scalar.copy, "w_se_bf", w_se_raw)
-        w_lo_bf = cast_dealt(nc.scalar.copy, "w_lo_bf", w_lo_raw)
-        nc.scalar.activation(out=hi_own2[:], in_=hi_own[:], func=ACT.Copy, scale=-2.0)
+        hi_own2 = sb("hi_own2", [P, PACK * V], F32, tag=None)
+        for i in range(2):
+            cols = slice(i * 2 * V, (i + 1) * 2 * V)
+            nc.gpsimd.tensor_scalar(out=hi_own2[:, cols], in0=hi_own[:, cols], scalar1=-2.0, scalar2=0.0, op0=ALU.mult, op1=ALU.add)
+        w_se_bf = cast_dealt(nc.scalar.copy, "w_se_bf", w_se_raw, None)
+        w_lo_bf = cast_dealt(nc.scalar.copy, "w_lo_bf", w_lo_raw, None)
+        hi_b = sb("hi_b", [P, PACK * V], F32, tag="w_se_raw")
+        gather(hi_b, y_hi, 0, pos2_t)
         w_se = mx_tiles("w_se", N)
         quantize(w_se, 0, w_se_bf)
-        y_se = [project("se", w_se, t, ACT.Relu, 1.0) for t in range(PACK)]
-        hi_b = sb("hi_b", [P, PACK * V], F32, tag="w_se_bf")
-        for t in range(PACK):
+        m_hi_bf = [cast(gpsimd_cast, "m_hi_bf0", m_hi_raw, 0, N // 2, "w_se_bf")]
+        y_se = [project("se", w_se, t, ACT.Relu, 1.0, 4096 if t == 0 else None) for t in range(PACK)]
+        for t in range(1, PACK):
             gather(hi_b, y_hi, t, pos2_t)
         hi_turned = [turn_sum([hi_a[:], hi_own2[:], hi_b[:]], h) for h in range(HALVES)]
         w_lo = mx_tiles("w_lo", N)
         quantize(w_lo, 0, w_lo_bf)
-        se = sb("se", [P, PACK * V], F32, tag="w_lo_bf")
+        m_se_bf = cast(gpsimd_cast, "m_se_bf", m_se_raw, 0, N, "w_lo_bf")
+        se = sb("se", [P, PACK * V], F32, tag=0)
         for t in range(PACK):
             gather(se, y_se, t, own_t)
-        m_hi_bf = cast(nc.scalar.copy, "m_hi_bf", m_hi_raw, 0, N, None)
-        m_se_bf = cast(nc.vector.tensor_copy, "m_se_bf", m_se_raw, 0, N, "se_y3")
-        z_hi = [turned_z("hi", hi_turned[h], h, ["se_y1", "se_y2"][h]) for h in range(HALVES)]
-        y_lo = [project("lo", w_lo, t, ACT.Copy, 0.5, "m_hi_raw" if t == 0 else None) for t in range(PACK)]
-        z_se = sb("se_z", [P, V * PACK], BF16, tag="gain_row")
-        nc.vector.tensor_tensor(
+        m_hi_bf.append(cast(nc.scalar.copy, "m_hi_bf1", m_hi_raw, N // 2, N, "se_y1"))
+        z_hi = [turned_z("hi", hi_turned[h], h, ["se_y2", "se_y3"][h]) for h in range(HALVES)]
+        y_lo = [project("lo", w_lo, t, ACT.Copy, 0.5, None if t == 0 else None) for t in range(PACK)]
+        z_se_rows = sb("se_z_rows", [P, PACK * V], BF16, tag=None)
+        for t in range(PACK):
+            cols = slice(t * V, (t + 1) * V)
+            nc.scalar.activation(out=z_se_rows[:, cols], in_=se[:, cols], func=ACT.Copy, scale=gain_t[:, t : t + 1])
+        z_se = sb("se_z", [P, V * PACK], BF16, tag=None)
+        nc.scalar.copy(
             out=z_se[:].rearrange("p (c i t) -> p c t i", i=4, t=PACK),
-            in0=se[:].rearrange("p (t c i) -> p c t i", t=PACK, i=4),
-            in1=gain_t[:].rearrange("p (c t i) -> p c t i", c=1, i=1).to_broadcast([P, V // 4, PACK, 4]),
-            op=ALU.mult,
+            in_=z_se_rows[:].rearrange("p (t c i) -> p c t i", t=PACK, i=4),
         )
         m_hi = mx_tiles("m_hi", N)
-        quantize(m_hi, 0, m_hi_bf)
+        for i in range(2):
+            quantize(m_hi, i * N // 2, m_hi_bf[i])
         z_hi_mx = mx_tiles("z_hi", V)
         for h in range(HALVES):
             quantize(z_hi_mx, h * P, z_hi[h])
-        z_se_mx = mx_tiles("z_se", V)
-        quantize(z_se_mx, 0, z_se)
-        m_se = mx_tiles("m_se", N)
-        quantize(m_se, 0, m_se_bf)
         num = [sum_banks.tile([P, PACK * P], F32, name="num%d" % h, tag="sum%d" % h) for h in range(HALVES)]
         den = [sum_banks.tile([P, PACK * P], F32, name="den%d" % h, tag="sum%d" % (2 + h)) for h in range(HALVES)]
+        m_lo_bf = cast(gpsimd_cast, "m_lo_bf", m_lo_raw, 0, N, 32768)
         e_hi = [weight("hi", z_hi_mx, m_hi, h) for h in range(HALVES)]
-        e_se = [weight("se", z_se_mx, m_se, h) for h in range(HALVES)]
-        m_lo_bf = cast(nc.scalar.copy, "m_lo_bf", m_lo_raw, 0, N, "se_th0")
-
-        lo_a = sb("lo_a", [P, PACK * V], F32, tag="gain_row")
+        lo_a = sb("lo_a", [P, PACK * V], F32, tag=28672)
         for t in range(PACK):
             gather(lo_a, y_lo, t, pos1_t)
 
@@ -278,24 +284,30 @@ def tile_picked_yacm_mix_p_kernel(
                 )
             return pre
 
-        lo_pre = [lo_sum(0, None)]
+        m_se = mx_tiles("m_se", N)
+        quantize(m_se, 0, m_se_bf)
+        z_se_mx = mx_tiles("z_se", V)
+        quantize(z_se_mx, 0, z_se)
+        m_lo = mx_tiles("m_lo", N)
+        quantize(m_lo, 0, m_lo_bf)
+        e_se = [weight("se", z_se_mx, m_se, h) for h in range(HALVES)]
+        lo_pre = [lo_sum(0, 20480)]
         z_lo_mx = mx_tiles("z_lo", V)
-        z_lo = direct_z("lo", lo_pre[0], 0, None)
-        p_hi = [mix("hi", dealt(hi_turned[h]), e_hi[h], h) for h in range(HALVES)]
-        quantize(z_lo_mx, 0, z_lo)
+        z_lo0 = direct_z("lo", lo_pre[0], 0, None)
+        p_hi = [mix("hi", dealt(hi_turned[h]), e_hi[h], h, [24576, 26624][h]) for h in range(HALVES)]
+        quantize(z_lo_mx, 0, z_lo0)
+        e_lo = [weight("lo", z_lo_mx, m_lo, 0)]
         se_turned = [turn_sum([se[:]], h) for h in range(HALVES)]
         for h in range(HALVES):
             turn_add(den[h], e_hi[h], True, False)
-        lo_pre.append(lo_sum(1, None))
-        m_lo = mx_tiles("m_lo", N)
-        quantize(m_lo, 0, m_lo_bf)
-        e_lo = [weight("lo", z_lo_mx, m_lo, 0)]
-        quantize(z_lo_mx, P, direct_z("lo", lo_pre[1], 1, "se_th0"))
+        lo_pre.append(lo_sum(1, 22528))
+        quantize(z_lo_mx, P, direct_z("lo", lo_pre[1], 1, 38400))
         e_lo.append(weight("lo", z_lo_mx, m_lo, 1))
         for h in range(HALVES):
             turn_add(num[h], p_hi[h], True, False)
+        for h in range(HALVES):
             turn_add(den[h], e_se[h], False, False)
-        p_se = [mix("se", plain(se_turned[h]), e_se[h], h, ["se_th0", "lo_z0"][h]) for h in range(HALVES)]
+        p_se = [mix("se", plain(se_turned[h]), e_se[h], h, [36864, 38912][h]) for h in range(HALVES)]
         lo_turned = [turn_sum([lo_pre[h][:]], h, mm_banks, "mm") for h in range(HALVES)]
         for h in range(HALVES):
             turn_add(den[h], e_lo[h], False, True)

@@ -19,6 +19,16 @@ ACT = mybir.ActivationFunctionType
 P = 128
 PACK = 4
 HALVES = V // P
+QUADRANTS = 4
+LINE = 4
+LIST_ROWS = 16
+KIB = 1024
+
+AT_W_LO_RAW, AT_SE, AT_SE_WINDOW = 0, 0, 4 * KIB
+AT_M_SE_RAW, AT_HI_PRODUCT = 8 * KIB, (8 * KIB, 10 * KIB)
+AT_M_LO_RAW, AT_LO_PRE = 20 * KIB, (20 * KIB, 22 * KIB)
+AT_LO_FIRST, AT_Z_SE, AT_M_LO_CAST = 28 * KIB, 31 * KIB, 32 * KIB
+AT_SE_PRODUCT, AT_Z_LO_LAST = (36 * KIB, 38 * KIB), 37 * KIB + KIB // 2
 
 
 def tile_picked_yacm_mix_p_kernel(
@@ -28,85 +38,93 @@ def tile_picked_yacm_mix_p_kernel(
     with ExitStack() as ctx:
         lists = ctx.enter_context(tc.tile_pool(name="lists", bufs=1))
         keep = ctx.enter_context(tc.tile_pool(name="keep", bufs=1))
-        mm_banks = ctx.enter_context(tc.psum_pool(name="mm_banks", bufs=2))
-        turn_banks = ctx.enter_context(tc.psum_pool(name="turn_banks", bufs=2))
+        work_banks = ctx.enter_context(tc.psum_pool(name="work_banks", bufs=1))
+        turn_banks = ctx.enter_context(tc.psum_pool(name="turn_banks", bufs=1))
         sum_banks = ctx.enter_context(tc.psum_pool(name="sum_banks", bufs=1))
+        shared = ctx.enter_context(tc.tile_pool(name="shared", bufs=1))
 
-        overlaid = ctx.enter_context(tc.tile_pool(name="overlaid", bufs=1))
+        def sb(name, shape, dtype, after=None, at=None):
+            if at is not None:
+                return shared.tile(shape, dtype, name=name, align_bytes=64, offset=at)
+            return keep.tile(shape, dtype, name=name, tag=after or name, align_bytes=64)
 
-        def sb(name, shape, dtype, tag=None):
-            if isinstance(tag, int):
-                return overlaid.tile(shape, dtype, name=name, align_bytes=64, offset=tag)
-            return keep.tile(shape, dtype, name=name, tag=tag or name, align_bytes=64)
+        def work_bank(name, h, width):
+            return work_banks.tile([P, width], F32, name=name, tag="work%d" % h)
+
+        def sum_bank(name, i):
+            return sum_banks.tile([P, PACK * P], F32, name=name, tag="sum%d" % i)
 
         def load_list(name, src):
             tile = lists.tile([P, src.shape[1]], U16, name=name)
             nc.sync.dma_start(out=tile[:], in_=src)
             return tile
 
-        def load_rows(name, src, c0, c1, tag=None):
-            raw = sb(name, [P, PACK, c1 - c0], F32, tag=tag)
+        def load_rows(name, src, c0=0, c1=N, at=None):
+            raw = sb(name, [P, PACK, c1 - c0], F32, at=at)
             nc.sync.dma_start(out=raw[:], in_=src.rearrange("(p j) c -> p j c", j=PACK)[:, :, c0:c1])
             return raw
 
-        warm_in = sb("warm_in", [P, 1], F32)
-        warm_out = sb("warm_out", [P, 1], F32)
-        nc.vector.memset(warm_in[:], 0.0)
-        nc.scalar.activation(out=warm_out[:], in_=warm_in[:], func=ACT.Tanh)
+        zero_in = sb("zero_in", [P, 1], F32)
+        zero = sb("zero", [P, 1], F32)
+        nc.vector.memset(zero_in[:], 0.0)
+        nc.scalar.activation(out=zero[:], in_=zero_in[:], func=ACT.Tanh)
 
         scale_table = sb("scale_table", [P, T], U8)
         nc.vector.memset(scale_table[:].bitcast(I32), 0)
-
         scale_rows = sb("scale_rows", [P, T // 4], I32)
-        for q in range(4):
+        for q in range(QUADRANTS):
             nc.sync.dma_start(out=scale_rows[32 * q : 32 * q + 4, :], in_=x_scales[0, 4 * q : 4 * q + 4, :].bitcast(I32))
         offs_t = load_list("offs_t", offs)
         gain_t = sb("gain_t", [P, PACK], F32)
         nc.sync.dma_start(out=gain_t[:], in_=gain.rearrange("(p t) o -> p (t o)", t=PACK))
-        w_hi_cuts = [0, P, 2 * P, N]
-        w_hi_raw = [load_rows("w_hi_raw0", w2, 0, w_hi_cuts[1])] if False else []
         word_table = sb("word_table", [P, T], U32)
         nc.sync.dma_start(out=word_table[:].bitcast(I32), in_=x_words[0].rearrange("p n t -> p (n t)").bitcast(I32))
-        w_hi_raw += [load_rows("w_hi_raw%d" % c0, w2, c0, c1) for c0, c1 in list(zip(w_hi_cuts, w_hi_cuts[1:]))[len(w_hi_raw):]]
+        w_hi_cuts = [0, P, 2 * P, N]
+        w_hi_raw = [load_rows("w_hi_raw%d" % c0, w2, c0, c1) for c0, c1 in zip(w_hi_cuts, w_hi_cuts[1:])]
         own_t = load_list("own_t", own)
         pos1_t = load_list("pos1_t", pos1)
         pos2_t = load_list("pos2_t", pos2)
-        w_se_raw = load_rows("w_se_raw", w3, 0, N)
-        w_lo_raw = load_rows("w_lo_raw", w1, 0, N, 0)
-        m_hi_raw = load_rows("m_hi_raw", m2, 0, N)
-        m_se_raw = load_rows("m_se_raw", m3, 0, N, 12288)
-        m_lo_raw = load_rows("m_lo_raw", m1, 0, N, 20480)
+        w_se_raw = load_rows("w_se_raw", w3)
+        w_lo_raw = load_rows("w_lo_raw", w1, at=AT_W_LO_RAW)
+        m_hi_raw = load_rows("m_hi_raw", m2)
+        m_se_raw = load_rows("m_se_raw", m3, at=AT_M_SE_RAW)
+        m_lo_raw = load_rows("m_lo_raw", m1, at=AT_M_LO_RAW)
 
         ident = sb("ident", [P, P], F32)
         make_identity(nc, ident[:])
 
-        for q in range(4):
-            nc.vector.tensor_copy(out=scale_table[32 * q : 32 * q + 4, :].bitcast(I32), in_=scale_rows[32 * q : 32 * q + 4, :])
+        for q in range(QUADRANTS):
+            rows = slice(32 * q, 32 * q + 4)
+            nc.vector.tensor_copy(out=scale_table[rows, :].bitcast(I32), in_=scale_rows[rows, :])
         x_codes = sb("x_codes", [P, S], U32)
         x_exps = sb("x_exps", [P, S], U8)
         nc.vector.tensor_copy(out=x_exps[:], in_=scale_table[:].indirect(offs_t[:]))
         nc.vector.tensor_copy(out=x_codes[:], in_=word_table[:].indirect(offs_t[:]))
 
-        def gpsimd_cast(out, in_):
+        def gpsimd_scale(out, in_, factor):
             half = out.shape[1] // 2
             for i in range(2):
                 cols = slice(i * half, (i + 1) * half)
-                nc.gpsimd.tensor_scalar(out=out[:, cols], in0=in_[:, cols], scalar1=1.0, scalar2=0.0, op0=ALU.mult, op1=ALU.add)
+                nc.gpsimd.tensor_scalar(
+                    out=out[:, cols], in0=in_[:, cols], scalar1=factor, scalar2=0.0, op0=ALU.mult, op1=ALU.add
+                )
 
-        def cast_dealt(copy, name, raw, tag=None):
-            grouped = sb(name, [P, N * PACK], BF16, tag=tag)
+        def gpsimd_copy(out, in_):
+            gpsimd_scale(out, in_, 1.0)
+
+        def cast(copy, name, raw, c0=0, c1=N, after=None, at=None):
+            grouped = sb(name, [P, (c1 - c0) * PACK], BF16, after, at)
             copy(
-                out=grouped[:].rearrange("p (t m j) -> p m t j", t=PACK, j=PACK),
-                in_=raw[:].rearrange("p j (m t) -> p m t j", t=PACK),
+                out=grouped[:].rearrange("p (c i j) -> p c j i", i=LINE, j=PACK),
+                in_=raw[:, :, c0:c1].rearrange("p j (c i) -> p c j i", i=LINE),
             )
             return grouped
 
-        def cast(copy, name, raw, c0=0, c1=None, tag=None):
-            c1 = c1 or raw.shape[2]
-            grouped = sb(name, [P, (c1 - c0) * PACK], BF16, tag=tag)
-            copy(
-                out=grouped[:].rearrange("p (c i j) -> p c j i", i=4, j=PACK),
-                in_=raw[:, :, c0:c1].rearrange("p j (c i) -> p c j i", i=4),
+        def cast_dealt(name, raw):
+            grouped = sb(name, [P, N * PACK], BF16)
+            nc.scalar.copy(
+                out=grouped[:].rearrange("p (t m j) -> p m t j", t=PACK, j=PACK),
+                in_=raw[:].rearrange("p j (m t) -> p m t j", t=PACK),
             )
             return grouped
 
@@ -117,28 +135,172 @@ def tile_picked_yacm_mix_p_kernel(
             c1 = c0 + grouped.shape[1] // PACK
             nc.vector.quantize_mx(out=mx[0][:, c0:c1].bitcast(FP8X4), scales=mx[1][:, c0:c1], in_=grouped[:])
 
-        def project(name, mx, t, func, scale, tag=None):
-            bank = sum_banks.tile([P, S], F32, name="y_bank", tag="sum%d" % t)
-            cols = slice(t * P, (t + 1) * P)
+        def product(bank, still, i, moving):
+            cols = slice(i * P, (i + 1) * P)
             nc.tensor.matmul_mx(
-                out=bank[:], lhsT=mx[0][:, cols].bitcast(FP8X4), lhsT_scale=mx[1][:, cols],
-                rhs=x_codes[:].bitcast(FP8X4), rhs_scale=x_exps[:], start=True, stop=True,
+                out=bank[:], lhsT=still[0][:, cols].bitcast(FP8X4), lhsT_scale=still[1][:, cols],
+                rhs=moving[0][:].bitcast(FP8X4), rhs_scale=moving[1][:], start=True, stop=True,
             )
-            window = sb("%s_y%d" % (name, t), [P, S], F32, tag=tag)
-            nc.scalar.activation(out=window[:], in_=bank[:], func=func, scale=scale)
+
+        def project(name, w_mx, t, bank, func, at=None, **affine):
+            product(bank, w_mx, t, (x_codes, x_exps))
+            window = sb("%s_y%d" % (name, t), [P, S], F32, at=at)
+            nc.scalar.activation(out=window[:], in_=bank[:], func=func, **affine)
             return window
 
-        def gather(dst, windows, t, offsets, h=None):
-            if h is None:
-                nc.vector.tensor_copy(out=dst[:, t * V : (t + 1) * V], in_=windows[t][:].indirect(offsets[:]))
-            else:
-                nc.vector.tensor_copy(
-                    out=dst[:, t * V + h * P : t * V + (h + 1) * P],
-                    in_=windows[t][:].indirect(offsets[:, h * P // 16 : (h + 1) * P // 16]),
+        def gather(dst, windows, t, offsets):
+            nc.vector.tensor_copy(out=dst[:, t * V : (t + 1) * V], in_=windows[t][:].indirect(offsets[:]))
+
+        def half_of(upright, h):
+            return upright[:].rearrange("p (t v) -> p t v", t=PACK)[:, :, h * P : (h + 1) * P]
+
+        def by_tile(turned):
+            return turned[:].rearrange("p (t m) -> p t m", t=PACK)
+
+        def as_dealt(turned):
+            return turned[:].rearrange("p (m t) -> p t m", t=PACK)
+
+        def turn_add(bank, blocks, first, last):
+            for t in range(PACK):
+                nc.tensor.matmul(
+                    out=bank[:, t * P : (t + 1) * P], lhsT=blocks[:, t, :], rhs=ident[:],
+                    is_transpose=True, start=(first and t == 0), stop=(last and t == PACK - 1),
                 )
 
-        def direct_z(name, pre, h, tag=None):
-            z = sb("%s_z%d" % (name, h), [P, P * PACK], BF16, tag=tag)
+        def turn_sum(terms, h):
+            bank = turn_banks.tile([P, N], F32, name="turned", tag="turn%d" % h)
+            for i, blocks in enumerate(terms):
+                turn_add(bank, blocks, i == 0, i == len(terms) - 1)
+            return bank
+
+        def weight(name, z_mx, m_mx, h):
+            bank = work_bank("logits", h, N)
+            product(bank, z_mx, h, m_mx)
+            th = sb("%s_th%d" % (name, h), [P, N], F32)
+            nc.scalar.activation(out=by_tile(th), in_=as_dealt(bank), func=ACT.Tanh, scale=0.5)
+            e = sb("%s_e%d" % (name, h), [P, N], F32)
+            nc.scalar.activation(out=e[:], in_=th[:], func=ACT.Exp, scale=0.5)
+            return e
+
+        def mix(name, pre_turned, e, h, at=None):
+            prod = sb("%s_p%d" % (name, h), [P, N], F32, at=at)
+            nc.vector.scalar_tensor_tensor(
+                out=by_tile(prod), in0=pre_turned, scalar=0.0, in1=by_tile(e), op0=ALU.max, op1=ALU.mult
+            )
+            return prod
+
+        gain_bank = work_bank("gain_bank", 0, N)
+        for t in range(PACK):
+            nc.tensor.transpose(gain_bank[:, t * P : (t + 1) * P], gain_t[:, t : t + 1].to_broadcast([P, P]), ident[:])
+        gain_row = sb("gain_row", [P, N], F32)
+        nc.scalar.copy(
+            out=gain_row[:].rearrange("p (m t) -> p m t", t=PACK), in_=gain_bank[:].rearrange("p (t m) -> p m t", t=PACK)
+        )
+
+        w_hi = mx_tiles("w_hi", N)
+        y_hi = []
+        for c0, raw in zip(w_hi_cuts, w_hi_raw):
+            copy = nc.vector.tensor_copy if c0 == w_hi_cuts[-2] else nc.scalar.copy
+            for c in range(0, raw.shape[2], P):
+                t = (c0 + c) // P
+                quantize(w_hi, c0 + c, cast(copy, "w_hi_bf%d" % t, raw, c, c + P))
+                y_hi.append(project("hi", w_hi, t, sum_bank("y_hi", t), ACT.Copy, scale=-0.5))
+        hi_first = sb("hi_first", [P, PACK * V], F32)
+        hi_own = sb("hi_own", [P, PACK * V], F32)
+        for t in range(PACK):
+            gather(hi_own, y_hi, t, own_t)
+            gather(hi_first, y_hi, t, pos1_t)
+        hi_centre = sb("hi_centre", [P, PACK * V], F32)
+        gpsimd_scale(hi_centre[:], hi_own[:], -2.0)
+
+        w_se_bf = cast_dealt("w_se_bf", w_se_raw)
+        w_lo_bf = cast_dealt("w_lo_bf", w_lo_raw)
+        hi_second = sb("hi_second", [P, PACK * V], F32, after="w_se_raw")
+        gather(hi_second, y_hi, 0, pos2_t)
+        w_se = mx_tiles("w_se", N)
+        quantize(w_se, 0, w_se_bf)
+        m_hi_bf = [cast(gpsimd_copy, "m_hi_bf0", m_hi_raw, 0, N // 2, after="w_se_bf")]
+        y_se = [
+            project("se", w_se, t, sum_bank("y_se", t), ACT.Relu, AT_SE_WINDOW if t == 0 else None, bias=zero[:])
+            for t in range(PACK)
+        ]
+        for t in range(1, PACK):
+            gather(hi_second, y_hi, t, pos2_t)
+        hi_turned = [turn_sum([half_of(x, h) for x in (hi_first, hi_second, hi_centre)], h) for h in range(HALVES)]
+
+        w_lo = mx_tiles("w_lo", N)
+        quantize(w_lo, 0, w_lo_bf)
+        m_se_bf = cast(gpsimd_copy, "m_se_bf", m_se_raw, after="w_lo_bf")
+        se = sb("se", [P, PACK * V], F32, at=AT_SE)
+        for t in range(PACK):
+            gather(se, y_se, t, own_t)
+        m_hi_bf.append(cast(nc.scalar.copy, "m_hi_bf1", m_hi_raw, N // 2, N, after="se_y1"))
+
+        z_hi = []
+        for h in range(HALVES):
+            z_turned = sb("hi_zt%d" % h, [P, N], BF16, after="se_y%d" % (2 + h))
+            nc.vector.scalar_tensor_tensor(
+                out=z_turned[:], in0=hi_turned[h][:], scalar=0.0, in1=gain_row[:], op0=ALU.max, op1=ALU.mult
+            )
+            pairs = work_bank("pairs", h, 2 * P)
+            for u in range(2):
+                nc.tensor.transpose(pairs[:, u * P : (u + 1) * P], z_turned[:].bitcast(F32)[:, u : N // 2 : 2], ident[:])
+            z = sb("hi_z%d" % h, [P, P * PACK], BF16)
+            nc.scalar.copy(
+                out=z[:].bitcast(F32).rearrange("p (v u) -> p v u", u=2), in_=pairs[:].rearrange("p (u v) -> p v u", u=2)
+            )
+            z_hi.append(z)
+
+        y_lo = [
+            project("lo", w_lo, t, sum_bank("y_lo", t) if t < HALVES else work_bank("y_lo", t - HALVES, S), ACT.Copy, scale=0.5)
+            for t in range(PACK)
+        ]
+        m_hi = mx_tiles("m_hi", N)
+        for i, part in enumerate(m_hi_bf):
+            quantize(m_hi, i * N // 2, part)
+        z_se = sb("se_z", [P, V * PACK], BF16, at=AT_Z_SE)
+        nc.vector.tensor_tensor(
+            out=z_se[:].rearrange("p (c i t) -> p c t i", i=LINE, t=PACK),
+            in0=se[:].rearrange("p (t c i) -> p c t i", t=PACK, i=LINE),
+            in1=gain_t[:].rearrange("p (c t i) -> p c t i", c=1, i=1).to_broadcast([P, V // LINE, PACK, LINE]),
+            op=ALU.mult,
+        )
+        z_hi_mx = mx_tiles("z_hi", V)
+        for h in range(HALVES):
+            quantize(z_hi_mx, h * P, z_hi[h])
+        z_se_mx = mx_tiles("z_se", V)
+        quantize(z_se_mx, 0, z_se)
+
+        num = [sum_bank("num%d" % h, h) for h in range(HALVES)]
+        den = [sum_bank("den%d" % h, HALVES + h) for h in range(HALVES)]
+        m_lo_bf = cast(gpsimd_copy, "m_lo_bf", m_lo_raw, at=AT_M_LO_CAST)
+        e_hi = [weight("hi", z_hi_mx, m_hi, h) for h in range(HALVES)]
+        lo_first = sb("lo_first", [P, PACK * V], F32, at=AT_LO_FIRST)
+        for t in range(PACK):
+            gather(lo_first, y_lo, t, pos1_t)
+
+        m_se = mx_tiles("m_se", N)
+        quantize(m_se, 0, m_se_bf)
+        e_se = [weight("se", z_se_mx, m_se, h) for h in range(HALVES)]
+        p_hi = [mix("hi", as_dealt(hi_turned[h]), e_hi[h], h, AT_HI_PRODUCT[h]) for h in range(HALVES)]
+        m_lo = mx_tiles("m_lo", N)
+        quantize(m_lo, 0, m_lo_bf)
+        se_turned = [turn_sum([half_of(se, h)], h) for h in range(HALVES)]
+        for banks, terms, first in ((den, e_hi, True), (num, p_hi, True), (den, e_se, False)):
+            for h in range(HALVES):
+                turn_add(banks[h], by_tile(terms[h]), first, False)
+
+        z_lo_mx = mx_tiles("z_lo", V)
+        lo_pre, e_lo = [], []
+        for h in range(HALVES):
+            pre = sb("lo_pre%d" % h, [P, PACK * P], F32, at=AT_LO_PRE[h])
+            offsets = pos2_t[:, h * P // LIST_ROWS : (h + 1) * P // LIST_ROWS]
+            for t in range(PACK):
+                nc.vector.tensor_tensor(
+                    out=pre[:, t * P : (t + 1) * P], in0=y_lo[t][:].indirect(offsets),
+                    in1=lo_first[:, t * V + h * P : t * V + (h + 1) * P], op=ALU.add,
+                )
+            z = sb("lo_z%d" % h, [P, P * PACK], BF16, at=AT_Z_LO_LAST if h == HALVES - 1 else None)
             nc.vector.scalar_tensor_tensor(
                 out=z[:].rearrange("p (v t) -> p v t", t=PACK),
                 in0=pre[:].rearrange("p (t v) -> p v t", t=PACK),
@@ -146,186 +308,33 @@ def tile_picked_yacm_mix_p_kernel(
                 in1=gain_t[:].rearrange("p (o t) -> p o t", o=1).to_broadcast([P, P, PACK]),
                 op0=ALU.max, op1=ALU.mult,
             )
-            return z
+            quantize(z_lo_mx, h * P, z)
+            lo_pre.append(pre)
+            e_lo.append(weight("lo", z_lo_mx, m_lo, h))
+            turn_add(den[h], by_tile(e_lo[h]), False, True)
 
-        def plain(bank):
-            return bank[:].rearrange("p (t m) -> p t m", t=PACK)
-
-        def turn_sum(terms, h, pool=turn_banks, tag="turn"):
-            bank = pool.tile([P, N], F32, name="turned", tag="%s%d" % (tag, h), bufs=1)
-            for i, term in enumerate(terms):
-                for t in range(PACK):
-                    nc.tensor.matmul(
-                        out=bank[:, t * P : (t + 1) * P], lhsT=term.rearrange("p (t v) -> p t v", t=PACK)[:, t, h * P % (term.shape[1] // PACK) :][:, :P], rhs=ident[:],
-                        is_transpose=True, start=(i == 0 and t == 0), stop=(i == len(terms) - 1 and t == PACK - 1),
-                    )
-            return bank
-
-        def turned_z(name, turned, h, tag=None):
-            zt = sb("%s_zt%d" % (name, h), [P, N], BF16, tag=tag)
-            nc.vector.scalar_tensor_tensor(
-                out=zt[:], in0=turned[:], scalar=0.0, in1=gain_row[:], op0=ALU.max, op1=ALU.mult
-            )
-            bank = mm_banks.tile([P, 2 * P], F32, name="pairs", tag="mm%d" % h, bufs=1)
-            for u in range(2):
-                nc.tensor.transpose(bank[:, u * P : (u + 1) * P], zt[:].bitcast(F32)[:, u : N // 2 : 2], ident[:])
-            z = sb("%s_z%d" % (name, h), [P, P * PACK], BF16, tag=[None, 32256][h])
-            nc.scalar.copy(
-                out=z[:].bitcast(F32).rearrange("p (v u) -> p v u", u=2), in_=bank[:].rearrange("p (u v) -> p v u", u=2)
-            )
-            return z
-
-        def weight(name, z_mx, m_mx, h):
-            bank = mm_banks.tile([P, N], F32, name="mm", tag="mm%d" % h, bufs=1)
-            cols = slice(h * P, (h + 1) * P)
-            nc.tensor.matmul_mx(
-                out=bank[:], lhsT=z_mx[0][:, cols].bitcast(FP8X4), lhsT_scale=z_mx[1][:, cols],
-                rhs=m_mx[0][:].bitcast(FP8X4), rhs_scale=m_mx[1][:], start=True, stop=True,
-            )
-            th = sb("%s_th%d" % (name, h), [P, N], F32)
-            nc.scalar.activation(
-                out=th[:].rearrange("p (t m) -> p t m", t=PACK), in_=bank[:].rearrange("p (m t) -> p t m", t=PACK),
-                func=ACT.Tanh, scale=0.5,
-            )
-            e = sb("%s_e%d" % (name, h), [P, N], F32)
-            nc.scalar.activation(out=e[:], in_=th[:], func=ACT.Exp, scale=0.5)
-            return e
-
-        def turn_add(bank, src, first, last):
-            for t in range(PACK):
-                nc.tensor.matmul(
-                    out=bank[:, t * P : (t + 1) * P], lhsT=src[:, t * P : (t + 1) * P], rhs=ident[:],
-                    is_transpose=True, start=(first and t == 0), stop=(last and t == PACK - 1),
-                )
-
-        def mix(name, turned, e, h, tag=None):
-            prod = sb("%s_p%d" % (name, h), [P, N], F32, tag=tag)
-            nc.vector.scalar_tensor_tensor(
-                out=prod[:].rearrange("p (t m) -> p t m", t=PACK), in0=turned, scalar=0.0,
-                in1=e[:].rearrange("p (t m) -> p t m", t=PACK), op0=ALU.max, op1=ALU.mult,
-            )
-            return prod
-
-        def dealt(bank):
-            return bank[:].rearrange("p (m t) -> p t m", t=PACK)
-
-        gain_bank = mm_banks.tile([P, N], F32, name="gain_bank", tag="mm0", bufs=1)
-        for t in range(PACK):
-            nc.tensor.transpose(gain_bank[:, t * P : (t + 1) * P], gain_t[:, t : t + 1].to_broadcast([P, P]), ident[:])
-
-        gain_row = sb("gain_row", [P, N], F32)
-        nc.scalar.copy(out=gain_row[:].rearrange("p (m t) -> p m t", t=PACK), in_=gain_bank[:].rearrange("p (t m) -> p m t", t=PACK))
-
-        w_hi = mx_tiles("w_hi", N)
-        y_hi = []
-        for c0, raw in zip(w_hi_cuts, w_hi_raw):
-            for c in range(0, raw.shape[2], P):
-                t = (c0 + c) // P
-                quantize(w_hi, c0 + c, cast(nc.scalar.copy if t < 2 else nc.vector.tensor_copy, "w_hi_bf%d" % t, raw, c, c + P))
-                y_hi.append(project("hi", w_hi, t, ACT.Copy, -0.5))
-        hi_a = sb("hi_a", [P, PACK * V], F32)
-        hi_own = sb("hi_own", [P, PACK * V], F32)
-        for t in range(PACK):
-            gather(hi_own, y_hi, t, own_t)
-            gather(hi_a, y_hi, t, pos1_t)
-        hi_own2 = sb("hi_own2", [P, PACK * V], F32, tag=None)
-        for i in range(2):
-            cols = slice(i * 2 * V, (i + 1) * 2 * V)
-            nc.gpsimd.tensor_scalar(out=hi_own2[:, cols], in0=hi_own[:, cols], scalar1=-2.0, scalar2=0.0, op0=ALU.mult, op1=ALU.add)
-        w_se_bf = cast_dealt(nc.scalar.copy, "w_se_bf", w_se_raw, None)
-        w_lo_bf = cast_dealt(nc.scalar.copy, "w_lo_bf", w_lo_raw, None)
-        hi_b = sb("hi_b", [P, PACK * V], F32, tag="w_se_raw")
-        gather(hi_b, y_hi, 0, pos2_t)
-        w_se = mx_tiles("w_se", N)
-        quantize(w_se, 0, w_se_bf)
-        m_hi_bf = [cast(gpsimd_cast, "m_hi_bf0", m_hi_raw, 0, N // 2, "w_se_bf")]
-        y_se = [project("se", w_se, t, ACT.Relu, 1.0, 4096 if t == 0 else None) for t in range(PACK)]
-        for t in range(1, PACK):
-            gather(hi_b, y_hi, t, pos2_t)
-        hi_turned = [turn_sum([hi_a[:], hi_own2[:], hi_b[:]], h) for h in range(HALVES)]
-        w_lo = mx_tiles("w_lo", N)
-        quantize(w_lo, 0, w_lo_bf)
-        m_se_bf = cast(gpsimd_cast, "m_se_bf", m_se_raw, 0, N, "w_lo_bf")
-        se = sb("se", [P, PACK * V], F32, tag=0)
-        for t in range(PACK):
-            gather(se, y_se, t, own_t)
-        m_hi_bf.append(cast(nc.scalar.copy, "m_hi_bf1", m_hi_raw, N // 2, N, "se_y1"))
-        z_hi = [turned_z("hi", hi_turned[h], h, ["se_y2", "se_y3"][h]) for h in range(HALVES)]
-        y_lo = [project("lo", w_lo, t, ACT.Copy, 0.5, None if t == 0 else None) for t in range(PACK)]
-        z_se_rows = sb("se_z_rows", [P, PACK * V], BF16, tag=None)
-        for t in range(PACK):
-            cols = slice(t * V, (t + 1) * V)
-            nc.scalar.activation(out=z_se_rows[:, cols], in_=se[:, cols], func=ACT.Copy, scale=gain_t[:, t : t + 1])
-        z_se = sb("se_z", [P, V * PACK], BF16, tag=None)
-        nc.scalar.copy(
-            out=z_se[:].rearrange("p (c i t) -> p c t i", i=4, t=PACK),
-            in_=z_se_rows[:].rearrange("p (t c i) -> p c t i", t=PACK, i=4),
-        )
-        m_hi = mx_tiles("m_hi", N)
-        for i in range(2):
-            quantize(m_hi, i * N // 2, m_hi_bf[i])
-        z_hi_mx = mx_tiles("z_hi", V)
+        p_se = [mix("se", by_tile(se_turned[h]), e_se[h], h, AT_SE_PRODUCT[h]) for h in range(HALVES)]
+        lo_turned = [turn_sum([by_tile(lo_pre[h])], h) for h in range(HALVES)]
         for h in range(HALVES):
-            quantize(z_hi_mx, h * P, z_hi[h])
-        num = [sum_banks.tile([P, PACK * P], F32, name="num%d" % h, tag="sum%d" % h) for h in range(HALVES)]
-        den = [sum_banks.tile([P, PACK * P], F32, name="den%d" % h, tag="sum%d" % (2 + h)) for h in range(HALVES)]
-        m_lo_bf = cast(gpsimd_cast, "m_lo_bf", m_lo_raw, 0, N, 32768)
-        e_hi = [weight("hi", z_hi_mx, m_hi, h) for h in range(HALVES)]
-        lo_a = sb("lo_a", [P, PACK * V], F32, tag=28672)
-        for t in range(PACK):
-            gather(lo_a, y_lo, t, pos1_t)
-
-        def lo_sum(h, tag):
-            pre = sb("lo_pre%d" % h, [P, PACK * P], F32, tag=tag)
-            for t in range(PACK):
-                nc.vector.tensor_tensor(
-                    out=pre[:, t * P : (t + 1) * P], in0=y_lo[t][:].indirect(pos2_t[:, h * P // 16 : (h + 1) * P // 16]),
-                    in1=lo_a[:, t * V + h * P : t * V + (h + 1) * P], op=ALU.add,
-                )
-            return pre
-
-        m_se = mx_tiles("m_se", N)
-        quantize(m_se, 0, m_se_bf)
-        z_se_mx = mx_tiles("z_se", V)
-        quantize(z_se_mx, 0, z_se)
-        m_lo = mx_tiles("m_lo", N)
-        quantize(m_lo, 0, m_lo_bf)
-        e_se = [weight("se", z_se_mx, m_se, h) for h in range(HALVES)]
-        lo_pre = [lo_sum(0, 20480)]
-        z_lo_mx = mx_tiles("z_lo", V)
-        z_lo0 = direct_z("lo", lo_pre[0], 0, None)
-        p_hi = [mix("hi", dealt(hi_turned[h]), e_hi[h], h, [24576, 26624][h]) for h in range(HALVES)]
-        quantize(z_lo_mx, 0, z_lo0)
-        e_lo = [weight("lo", z_lo_mx, m_lo, 0)]
-        se_turned = [turn_sum([se[:]], h) for h in range(HALVES)]
-        for h in range(HALVES):
-            turn_add(den[h], e_hi[h], True, False)
-        lo_pre.append(lo_sum(1, 22528))
-        quantize(z_lo_mx, P, direct_z("lo", lo_pre[1], 1, 38400))
-        e_lo.append(weight("lo", z_lo_mx, m_lo, 1))
-        for h in range(HALVES):
-            turn_add(num[h], p_hi[h], True, False)
-        for h in range(HALVES):
-            turn_add(den[h], e_se[h], False, False)
-        p_se = [mix("se", plain(se_turned[h]), e_se[h], h, [36864, 38912][h]) for h in range(HALVES)]
-        lo_turned = [turn_sum([lo_pre[h][:]], h, mm_banks, "mm") for h in range(HALVES)]
-        for h in range(HALVES):
-            turn_add(den[h], e_lo[h], False, True)
-            turn_add(num[h], p_se[h], False, False)
-        for h in range(HALVES):
-            p_lo = mix("lo", plain(lo_turned[h]), e_lo[h], h)
-            turn_add(num[h], p_lo, False, True)
+            turn_add(num[h], by_tile(p_se[h]), False, False)
+            p_lo = mix("lo", by_tile(lo_turned[h]), e_lo[h], h)
+            turn_add(num[h], by_tile(p_lo), False, True)
 
         out_rows = out.rearrange("(p t) v -> p t v", t=PACK)
+        root = [sb("root%d" % h, [P, PACK * P], F32, after="lo_th%d" % (1 - h)) for h in range(HALVES)]
+        num_root = sb("num_root", [P, PACK * P], F32)
+        inverse = sb("inverse", [P, PACK * P], F32)
+        pieces = [slice(i * 2 * P, (i + 1) * 2 * P) for i in range(2)]
         for h in range(HALVES):
-            root = sb("root%d" % h, [P, PACK * P], F32, tag="lo_th%d" % (1 - h))
-            nc.scalar.activation(out=root[:], in_=den[h][:], func=ACT.Abs_reciprocal_sqrt)
-            once = sb("once%d" % h, [P, PACK * P], F32)
-            res = sb("res%d" % h, [P, PACK * P], F32)
-            if h == 0:
-                nc.vector.tensor_tensor(out=once[:], in0=num[h][:], in1=root[:], op=ALU.mult)
-                nc.vector.tensor_tensor(out=res[:], in0=once[:], in1=root[:], op=ALU.mult)
-            else:
-                nc.scalar.activation(out=once[:], in_=root[:], func=ACT.Square)
-                nc.vector.tensor_tensor(out=res[:], in0=num[h][:], in1=once[:], op=ALU.mult)
-            nc.sync.dma_start(out=out_rows[:, :, h * P : (h + 1) * P], in_=res[:].rearrange("p (t v) -> p t v", t=PACK))
+            for cols in pieces:
+                nc.scalar.activation(out=root[h][:, cols], in_=den[h][:, cols], func=ACT.Abs_reciprocal_sqrt)
+        for cols in pieces:
+            nc.vector.tensor_tensor(out=num_root[:, cols], in0=num[0][:, cols], in1=root[0][:, cols], op=ALU.mult)
+            nc.scalar.activation(out=inverse[:, cols], in_=root[1][:, cols], func=ACT.Square)
+        for h, (left, right) in enumerate(((num_root, root[0]), (num[1], inverse))):
+            for i, cols in enumerate(pieces):
+                res = sb("res%d_%d" % (h, i), [P, 2 * P], F32)
+                nc.vector.tensor_tensor(out=res[:], in0=left[:, cols], in1=right[:, cols], op=ALU.mult)
+                nc.sync.dma_start(
+                    out=out_rows[:, 2 * i : 2 * i + 2, h * P : (h + 1) * P], in_=res[:].rearrange("p (t v) -> p t v", t=2)
+                )

from contextlib import ExitStack

import concourse.mybir as mybir
from concourse.masks import make_identity

K, T, S, V, H, N = 512, 2048, 512, 256, 512, 512
FLOPS = 2 * 3 * K * N * S + 2 * 3 * H * N * V

F32 = mybir.dt.float32
BF16 = mybir.dt.bfloat16
I32 = mybir.dt.int32
U32 = mybir.dt.uint32
U16 = mybir.dt.uint16
U8 = mybir.dt.uint8
FP8X4 = mybir.dt.float8_e4m3fn_x4
ALU = mybir.AluOpType
ACT = mybir.ActivationFunctionType

P = 128
PACK = 4
HALVES = V // P
QUADRANTS = 4
LINE = 4
LIST_ROWS = 16
KIB = 1024

AT_W_LO_RAW, AT_SE, AT_SE_WINDOW = 0, 0, 4 * KIB
AT_M_SE_RAW, AT_HI_PRODUCT = 8 * KIB, (8 * KIB, 10 * KIB)
AT_M_LO_RAW, AT_LO_PRE = 20 * KIB, (20 * KIB, 22 * KIB)
AT_LO_FIRST, AT_Z_SE, AT_M_LO_CAST = 28 * KIB, 31 * KIB, 32 * KIB
AT_SE_PRODUCT, AT_Z_LO_LAST = (36 * KIB, 38 * KIB), 37 * KIB + KIB // 2


def tile_picked_yacm_mix_p_kernel(
    tc, x_words, x_scales, w1, w2, w3, gain, m1, m2, m3, offs, pos1, pos2, own, out
):
    nc = tc.nc
    with ExitStack() as ctx:
        lists = ctx.enter_context(tc.tile_pool(name="lists", bufs=1))
        keep = ctx.enter_context(tc.tile_pool(name="keep", bufs=1))
        work_banks = ctx.enter_context(tc.psum_pool(name="work_banks", bufs=1))
        turn_banks = ctx.enter_context(tc.psum_pool(name="turn_banks", bufs=1))
        sum_banks = ctx.enter_context(tc.psum_pool(name="sum_banks", bufs=1))
        shared = ctx.enter_context(tc.tile_pool(name="shared", bufs=1))

        def sb(name, shape, dtype, after=None, at=None):
            if at is not None:
                return shared.tile(shape, dtype, name=name, align_bytes=64, offset=at)
            return keep.tile(shape, dtype, name=name, tag=after or name, align_bytes=64)

        def work_bank(name, h, width):
            return work_banks.tile([P, width], F32, name=name, tag="work%d" % h)

        def sum_bank(name, i):
            return sum_banks.tile([P, PACK * P], F32, name=name, tag="sum%d" % i)

        def load_list(name, src):
            tile = lists.tile([P, src.shape[1]], U16, name=name)
            nc.sync.dma_start(out=tile[:], in_=src)
            return tile

        def load_rows(name, src, c0=0, c1=N, at=None):
            raw = sb(name, [P, PACK, c1 - c0], F32, at=at)
            nc.sync.dma_start(out=raw[:], in_=src.rearrange("(p j) c -> p j c", j=PACK)[:, :, c0:c1])
            return raw

        zero_in = sb("zero_in", [P, 1], F32)
        zero = sb("zero", [P, 1], F32)
        nc.vector.memset(zero_in[:], 0.0)
        nc.scalar.activation(out=zero[:], in_=zero_in[:], func=ACT.Tanh)

        scale_table = sb("scale_table", [P, T], U8)
        nc.vector.memset(scale_table[:].bitcast(I32), 0)
        scale_rows = sb("scale_rows", [P, T // 4], I32)
        for q in range(QUADRANTS):
            nc.sync.dma_start(out=scale_rows[32 * q : 32 * q + 4, :], in_=x_scales[0, 4 * q : 4 * q + 4, :].bitcast(I32))
        offs_t = load_list("offs_t", offs)
        gain_t = sb("gain_t", [P, PACK], F32)
        nc.sync.dma_start(out=gain_t[:], in_=gain.rearrange("(p t) o -> p (t o)", t=PACK))
        word_table = sb("word_table", [P, T], U32)
        nc.sync.dma_start(out=word_table[:].bitcast(I32), in_=x_words[0].rearrange("p n t -> p (n t)").bitcast(I32))
        w_hi_cuts = [0, P, 2 * P, N]
        w_hi_raw = [load_rows("w_hi_raw%d" % c0, w2, c0, c1) for c0, c1 in zip(w_hi_cuts, w_hi_cuts[1:])]
        own_t = load_list("own_t", own)
        pos1_t = load_list("pos1_t", pos1)
        pos2_t = load_list("pos2_t", pos2)
        w_se_raw = load_rows("w_se_raw", w3)
        w_lo_raw = load_rows("w_lo_raw", w1, at=AT_W_LO_RAW)
        m_hi_raw = load_rows("m_hi_raw", m2)
        m_se_raw = load_rows("m_se_raw", m3, at=AT_M_SE_RAW)
        m_lo_raw = load_rows("m_lo_raw", m1, at=AT_M_LO_RAW)

        ident = sb("ident", [P, P], F32)
        make_identity(nc, ident[:])

        for q in range(QUADRANTS):
            rows = slice(32 * q, 32 * q + 4)
            nc.vector.tensor_copy(out=scale_table[rows, :].bitcast(I32), in_=scale_rows[rows, :])
        x_codes = sb("x_codes", [P, S], U32)
        x_exps = sb("x_exps", [P, S], U8)
        nc.vector.tensor_copy(out=x_exps[:], in_=scale_table[:].indirect(offs_t[:]))
        nc.vector.tensor_copy(out=x_codes[:], in_=word_table[:].indirect(offs_t[:]))

        def gpsimd_scale(out, in_, factor):
            half = out.shape[1] // 2
            for i in range(2):
                cols = slice(i * half, (i + 1) * half)
                nc.gpsimd.tensor_scalar(
                    out=out[:, cols], in0=in_[:, cols], scalar1=factor, scalar2=0.0, op0=ALU.mult, op1=ALU.add
                )

        def gpsimd_copy(out, in_):
            gpsimd_scale(out, in_, 1.0)

        def cast(copy, name, raw, c0=0, c1=N, after=None, at=None):
            grouped = sb(name, [P, (c1 - c0) * PACK], BF16, after, at)
            copy(
                out=grouped[:].rearrange("p (c i j) -> p c j i", i=LINE, j=PACK),
                in_=raw[:, :, c0:c1].rearrange("p j (c i) -> p c j i", i=LINE),
            )
            return grouped

        def cast_dealt(name, raw):
            grouped = sb(name, [P, N * PACK], BF16)
            nc.scalar.copy(
                out=grouped[:].rearrange("p (t m j) -> p m t j", t=PACK, j=PACK),
                in_=raw[:].rearrange("p j (m t) -> p m t j", t=PACK),
            )
            return grouped

        def mx_tiles(name, width):
            return sb(name + "_codes", [P, width], U32), sb(name + "_exps", [P, width], U8)

        def quantize(mx, c0, grouped):
            c1 = c0 + grouped.shape[1] // PACK
            nc.vector.quantize_mx(out=mx[0][:, c0:c1].bitcast(FP8X4), scales=mx[1][:, c0:c1], in_=grouped[:])

        def product(bank, still, i, moving):
            cols = slice(i * P, (i + 1) * P)
            nc.tensor.matmul_mx(
                out=bank[:], lhsT=still[0][:, cols].bitcast(FP8X4), lhsT_scale=still[1][:, cols],
                rhs=moving[0][:].bitcast(FP8X4), rhs_scale=moving[1][:], start=True, stop=True,
            )

        def project(name, w_mx, t, bank, func, at=None, **affine):
            product(bank, w_mx, t, (x_codes, x_exps))
            window = sb("%s_y%d" % (name, t), [P, S], F32, at=at)
            nc.scalar.activation(out=window[:], in_=bank[:], func=func, **affine)
            return window

        def gather(dst, windows, t, offsets):
            nc.vector.tensor_copy(out=dst[:, t * V : (t + 1) * V], in_=windows[t][:].indirect(offsets[:]))

        def half_of(upright, h):
            return upright[:].rearrange("p (t v) -> p t v", t=PACK)[:, :, h * P : (h + 1) * P]

        def by_tile(turned):
            return turned[:].rearrange("p (t m) -> p t m", t=PACK)

        def as_dealt(turned):
            return turned[:].rearrange("p (m t) -> p t m", t=PACK)

        def turn_add(bank, blocks, first, last):
            for t in range(PACK):
                nc.tensor.matmul(
                    out=bank[:, t * P : (t + 1) * P], lhsT=blocks[:, t, :], rhs=ident[:],
                    is_transpose=True, start=(first and t == 0), stop=(last and t == PACK - 1),
                )

        def turn_sum(terms, h):
            bank = turn_banks.tile([P, N], F32, name="turned", tag="turn%d" % h)
            for i, blocks in enumerate(terms):
                turn_add(bank, blocks, i == 0, i == len(terms) - 1)
            return bank

        def weight(name, z_mx, m_mx, h):
            bank = work_bank("logits", h, N)
            product(bank, z_mx, h, m_mx)
            th = sb("%s_th%d" % (name, h), [P, N], F32)
            nc.scalar.activation(out=by_tile(th), in_=as_dealt(bank), func=ACT.Tanh, scale=0.5)
            e = sb("%s_e%d" % (name, h), [P, N], F32)
            nc.scalar.activation(out=e[:], in_=th[:], func=ACT.Exp, scale=0.5)
            return e

        def mix(name, pre_turned, e, h, at=None):
            prod = sb("%s_p%d" % (name, h), [P, N], F32, at=at)
            nc.vector.scalar_tensor_tensor(
                out=by_tile(prod), in0=pre_turned, scalar=0.0, in1=by_tile(e), op0=ALU.max, op1=ALU.mult
            )
            return prod

        gain_bank = work_bank("gain_bank", 0, N)
        for t in range(PACK):
            nc.tensor.transpose(gain_bank[:, t * P : (t + 1) * P], gain_t[:, t : t + 1].to_broadcast([P, P]), ident[:])
        gain_row = sb("gain_row", [P, N], F32)
        nc.scalar.copy(
            out=gain_row[:].rearrange("p (m t) -> p m t", t=PACK), in_=gain_bank[:].rearrange("p (t m) -> p m t", t=PACK)
        )

        w_hi = mx_tiles("w_hi", N)
        y_hi = []
        for c0, raw in zip(w_hi_cuts, w_hi_raw):
            copy = nc.vector.tensor_copy if c0 == w_hi_cuts[-2] else nc.scalar.copy
            for c in range(0, raw.shape[2], P):
                t = (c0 + c) // P
                quantize(w_hi, c0 + c, cast(copy, "w_hi_bf%d" % t, raw, c, c + P))
                y_hi.append(project("hi", w_hi, t, sum_bank("y_hi", t), ACT.Copy, scale=-0.5))
        hi_first = sb("hi_first", [P, PACK * V], F32)
        hi_own = sb("hi_own", [P, PACK * V], F32)
        for t in range(PACK):
            gather(hi_own, y_hi, t, own_t)
            gather(hi_first, y_hi, t, pos1_t)
        hi_centre = sb("hi_centre", [P, PACK * V], F32)
        gpsimd_scale(hi_centre[:], hi_own[:], -2.0)

        w_se_bf = cast_dealt("w_se_bf", w_se_raw)
        w_lo_bf = cast_dealt("w_lo_bf", w_lo_raw)
        hi_second = sb("hi_second", [P, PACK * V], F32, after="w_se_raw")
        gather(hi_second, y_hi, 0, pos2_t)
        w_se = mx_tiles("w_se", N)
        quantize(w_se, 0, w_se_bf)
        m_hi_bf = [cast(gpsimd_copy, "m_hi_bf0", m_hi_raw, 0, N // 2, after="w_se_bf")]
        y_se = [
            project("se", w_se, t, sum_bank("y_se", t), ACT.Relu, AT_SE_WINDOW if t == 0 else None, bias=zero[:])
            for t in range(PACK)
        ]
        for t in range(1, PACK):
            gather(hi_second, y_hi, t, pos2_t)
        hi_turned = [turn_sum([half_of(x, h) for x in (hi_first, hi_second, hi_centre)], h) for h in range(HALVES)]

        w_lo = mx_tiles("w_lo", N)
        quantize(w_lo, 0, w_lo_bf)
        m_se_bf = cast(gpsimd_copy, "m_se_bf", m_se_raw, after="w_lo_bf")
        se = sb("se", [P, PACK * V], F32, at=AT_SE)
        for t in range(PACK):
            gather(se, y_se, t, own_t)
        m_hi_bf.append(cast(nc.scalar.copy, "m_hi_bf1", m_hi_raw, N // 2, N, after="se_y1"))

        z_hi = []
        for h in range(HALVES):
            z_turned = sb("hi_zt%d" % h, [P, N], BF16, after="se_y%d" % (2 + h))
            nc.vector.scalar_tensor_tensor(
                out=z_turned[:], in0=hi_turned[h][:], scalar=0.0, in1=gain_row[:], op0=ALU.max, op1=ALU.mult
            )
            pairs = work_bank("pairs", h, 2 * P)
            for u in range(2):
                nc.tensor.transpose(pairs[:, u * P : (u + 1) * P], z_turned[:].bitcast(F32)[:, u : N // 2 : 2], ident[:])
            z = sb("hi_z%d" % h, [P, P * PACK], BF16)
            nc.scalar.copy(
                out=z[:].bitcast(F32).rearrange("p (v u) -> p v u", u=2), in_=pairs[:].rearrange("p (u v) -> p v u", u=2)
            )
            z_hi.append(z)

        y_lo = [
            project("lo", w_lo, t, sum_bank("y_lo", t) if t < HALVES else work_bank("y_lo", t - HALVES, S), ACT.Copy, scale=0.5)
            for t in range(PACK)
        ]
        m_hi = mx_tiles("m_hi", N)
        for i, part in enumerate(m_hi_bf):
            quantize(m_hi, i * N // 2, part)
        z_se = sb("se_z", [P, V * PACK], BF16, at=AT_Z_SE)
        nc.vector.tensor_tensor(
            out=z_se[:].rearrange("p (c i t) -> p c t i", i=LINE, t=PACK),
            in0=se[:].rearrange("p (t c i) -> p c t i", t=PACK, i=LINE),
            in1=gain_t[:].rearrange("p (c t i) -> p c t i", c=1, i=1).to_broadcast([P, V // LINE, PACK, LINE]),
            op=ALU.mult,
        )
        z_hi_mx = mx_tiles("z_hi", V)
        for h in range(HALVES):
            quantize(z_hi_mx, h * P, z_hi[h])
        z_se_mx = mx_tiles("z_se", V)
        quantize(z_se_mx, 0, z_se)

        num = [sum_bank("num%d" % h, h) for h in range(HALVES)]
        den = [sum_bank("den%d" % h, HALVES + h) for h in range(HALVES)]
        m_lo_bf = cast(gpsimd_copy, "m_lo_bf", m_lo_raw, at=AT_M_LO_CAST)
        e_hi = [weight("hi", z_hi_mx, m_hi, h) for h in range(HALVES)]
        lo_first = sb("lo_first", [P, PACK * V], F32, at=AT_LO_FIRST)
        for t in range(PACK):
            gather(lo_first, y_lo, t, pos1_t)

        m_se = mx_tiles("m_se", N)
        quantize(m_se, 0, m_se_bf)
        e_se = [weight("se", z_se_mx, m_se, h) for h in range(HALVES)]
        p_hi = [mix("hi", as_dealt(hi_turned[h]), e_hi[h], h, AT_HI_PRODUCT[h]) for h in range(HALVES)]
        m_lo = mx_tiles("m_lo", N)
        quantize(m_lo, 0, m_lo_bf)
        se_turned = [turn_sum([half_of(se, h)], h) for h in range(HALVES)]
        for banks, terms, first in ((den, e_hi, True), (num, p_hi, True), (den, e_se, False)):
            for h in range(HALVES):
                turn_add(banks[h], by_tile(terms[h]), first, False)

        z_lo_mx = mx_tiles("z_lo", V)
        lo_pre, e_lo = [], []
        for h in range(HALVES):
            pre = sb("lo_pre%d" % h, [P, PACK * P], F32, at=AT_LO_PRE[h])
            offsets = pos2_t[:, h * P // LIST_ROWS : (h + 1) * P // LIST_ROWS]
            for t in range(PACK):
                nc.vector.tensor_tensor(
                    out=pre[:, t * P : (t + 1) * P], in0=y_lo[t][:].indirect(offsets),
                    in1=lo_first[:, t * V + h * P : t * V + (h + 1) * P], op=ALU.add,
                )
            z = sb("lo_z%d" % h, [P, P * PACK], BF16, at=AT_Z_LO_LAST if h == HALVES - 1 else None)
            nc.vector.scalar_tensor_tensor(
                out=z[:].rearrange("p (v t) -> p v t", t=PACK),
                in0=pre[:].rearrange("p (t v) -> p v t", t=PACK),
                scalar=0.0,
                in1=gain_t[:].rearrange("p (o t) -> p o t", o=1).to_broadcast([P, P, PACK]),
                op0=ALU.max, op1=ALU.mult,
            )
            quantize(z_lo_mx, h * P, z)
            lo_pre.append(pre)
            e_lo.append(weight("lo", z_lo_mx, m_lo, h))
            turn_add(den[h], by_tile(e_lo[h]), False, True)

        p_se = [mix("se", by_tile(se_turned[h]), e_se[h], h, AT_SE_PRODUCT[h]) for h in range(HALVES)]
        lo_turned = [turn_sum([by_tile(lo_pre[h])], h) for h in range(HALVES)]
        for h in range(HALVES):
            turn_add(num[h], by_tile(p_se[h]), False, False)
            p_lo = mix("lo", by_tile(lo_turned[h]), e_lo[h], h)
            turn_add(num[h], by_tile(p_lo), False, True)

        out_rows = out.rearrange("(p t) v -> p t v", t=PACK)
        root = [sb("root%d" % h, [P, PACK * P], F32, after="lo_th%d" % (1 - h)) for h in range(HALVES)]
        num_root = sb("num_root", [P, PACK * P], F32)
        inverse = sb("inverse", [P, PACK * P], F32)
        pieces = [slice(i * 2 * P, (i + 1) * 2 * P) for i in range(2)]
        for h in range(HALVES):
            for cols in pieces:
                nc.scalar.activation(out=root[h][:, cols], in_=den[h][:, cols], func=ACT.Abs_reciprocal_sqrt)
        for cols in pieces:
            nc.vector.tensor_tensor(out=num_root[:, cols], in0=num[0][:, cols], in1=root[0][:, cols], op=ALU.mult)
            nc.scalar.activation(out=inverse[:, cols], in_=root[1][:, cols], func=ACT.Square)
        for h, (left, right) in enumerate(((num_root, root[0]), (num[1], inverse))):
            for i, cols in enumerate(pieces):
                res = sb("res%d_%d" % (h, i), [P, 2 * P], F32)
                nc.vector.tensor_tensor(out=res[:], in0=left[:, cols], in1=right[:, cols], op=ALU.mult)
                nc.sync.dma_start(
                    out=out_rows[:, 2 * i : 2 * i + 2, h * P : (h + 1) * P], in_=res[:].rearrange("p (t v) -> p t v", t=2)
                )
